import numpy as np, ml_dtypes
CORES = [24,25,26,27,28,29,30,31,224,225,226,227,228,229,230,231]
N = 16
T, KB = 2048, 16
CAPP = 256
def entries(a): return a.T.reshape(-1)
def pack(v, P): return np.ascontiguousarray(np.asarray(v, np.int32).reshape(-1, P).T)
def order(K):
    return np.argsort(K, kind="stable")
def most(K):
    o = order(K); return int(np.bincount(o // T * N + np.arange(N * T) // T, minlength=N * N).max())
def lists(rng, how):
    i, G = np.arange(N), T // CAPP
    if how == "uniform":
        for again in range(50):
            K = rng.integers(0, KB, (N, T))
            if most(K.reshape(-1)) <= CAPP: break
        else: K = np.broadcast_to(np.arange(T) % KB, (N, T)).copy()
    else:
        if how == "uneven":
            t = rng.integers(0, CAPP + 1, N)
            if t.sum() < T: t = CAPP - t
            t[0] = CAPP; w = np.diff(np.minimum(np.cumsum(t), T), prepend=0); L = w[(rng.permutation(N)[:, None] - rng.permutation(N)) % N]
        else:
            w = np.zeros(N, int); w[(G * (ord(how[-1]) - 97) + np.arange(G)) % N] = CAPP; L = w[(i[:, None] - i) % N]
        a = N - 1 - np.argmax(L[::-1] > 0, axis=0)
        m = np.minimum(rng.integers(1, CAPP, N - 1), L[a[:-1], i[1:]])
        v = np.nonzero((L[a[:-1], i[:-1]] == CAPP) & (L[a[:-1], i[1:]] == CAPP) & (a[:-1] != np.append(-1, a[:-2])))[0]
        if len(v): m[rng.choice(v)] = CAPP
        C = L.copy(); C[a[:-1], i[:-1]] += m; C[a[:-1], i[1:]] -= m
        kv = np.sort(rng.permutation(KB)[:N]); K = np.stack([rng.permutation(np.repeat(kv, c)) for c in C]); K[::3] = np.sort(K[::3], axis=1)
    return {"key": np.stack([pack(k, 16) for k in K])}
def setup_inputs(rng):
    return dict({"x": rng.standard_normal((N, 128, T), dtype=np.float32).astype(ml_dtypes.bfloat16)}, **lists(rng, "uniform"))
def setup_inputs_fulla(rng):
    d = setup_inputs(rng); d.update(lists(rng, "fulla"))
    for k in ("x",): d[k] = (d[k].astype(np.float32) * 1048576.0).astype(d[k].dtype)
    return d
def setup_inputs_fullb(rng):
    d = setup_inputs(rng); d.update(lists(rng, "fullb"))
    for k in ("x",): d[k] = (d[k].astype(np.float32) * (1 / 1024.0)).astype(d[k].dtype)
    return d
def setup_inputs_uneven(rng):
    d = setup_inputs(rng); d.update(lists(rng, "uneven"))
    return d
def check_inputs(x):
    bad = []
    if x["key"].min() < 0 or x["key"].max() >= KB: bad.append("key out of range")
    if most(np.concatenate([entries(a) for a in x["key"]])) > CAPP: bad.append("more than CAPP columns go from one rank to one rank")
    return bad
def reference(x, key):
    X = np.concatenate(list(x), axis=1); K = np.concatenate([entries(a) for a in key])
    Y = X[:, order(K)]
    return {"y": np.stack([Y[:, T * r:T * r + T] for r in range(N)])}

@@ -1,0 +1,401 @@
+import numpy as np
+from concourse.bass import DstId, RemoteDMATransfer
+from concourse.mybir import dt, AluOpType, AxisListType, ActivationFunctionType
+
+W = 2048
+SLOT = 272
+PIECES = [(0, 512), (512, 1024), (1024, 1536), (1536, 2048)]
+F, H, I, U, B = "float32", "float16", "int32", "uint16", "bfloat16"
+SCRATCH = {
+    "xs": ("sbuf", [128, W], B), "mx": ("sbuf", [128, W], B), "ys": ("sbuf", [128, W], B),
+    "so": ("sbuf", [128, 8 * SLOT], B), "sm": ("sbuf", [128, 8 * SLOT], B), "land": ("sbuf", [128, 16 * SLOT], B),
+    "ki": ("sbuf", [128, 128], I), "k16": ("sbuf", [128, 128], H),
+    "fs": ("sbuf", [128, 256], F), "is": ("sbuf", [128, 128], I),
+    "colm": ("sbuf", [128, 128], F), "colk": ("sbuf", [128, 128], F), "colq": ("sbuf", [128, 128], F), "dif": ("sbuf", [128, 128], F),
+    "oc": ("sbuf", [128, 32], H),
+    "colm16": ("sbuf", [128, 128], H), "colq16": ("sbuf", [128, 128], H),
+    "ones": ("sbuf", [128, 128], H), "mr": ("sbuf", [128, 128], H), "samem": ("sbuf", [128, 128], H), "samek": ("sbuf", [128, 128], H),
+    "ltk": ("sbuf", [128, 128], H), "nle": ("sbuf", [128, 128], H), "bm": ("sbuf", [128, 128], H),
+    "samekr": ("sbuf", [128, 128], H), "ltkr": ("sbuf", [128, 128], H), "um": ("sbuf", [128, 128], H), "ident": ("sbuf", [128, 128], H),
+    "selo": ("sbuf", [128, 128], H), "selm": ("sbuf", [128, 128], H),
+    "ee": ("sbuf", [128, 256], F), "em": ("sbuf", [128, 128], F), "fm": ("sbuf", [128, 128], F), "posc": ("sbuf", [128, 128], F),
+    "oh": ("sbuf", [128, 256], H), "sc": ("sbuf", [128, 256], H), "wb": ("sbuf", [128, 256], H), "ow": ("sbuf", [128, 256], H),
+    "lh": ("sbuf", [128, 2048], H), "rh": ("sbuf", [128, 2048], H),
+    "sl": ("sbuf", [128, 160], F), "slx": ("sbuf", [128, 160], F), "slu": ("sbuf", [128, 128], U), "slm": ("sbuf", [128, 128], U),
+    "lt": ("sbuf", [128, 64], F), "c16": ("sbuf", [128, 4], H), "cl": ("sbuf", [128, 32], H), "ou": ("sbuf", [128, 32], U),
+    "lown": ("sbuf", [128, 256], U), "lmir": ("sbuf", [128, 256], U),
+    "rl": ("sbuf", [128, 512], F), "ll": ("sbuf", [128, 512], F), "fi": ("sbuf", [128, 128], F), "fu": ("sbuf", [128, 128], U),
+}
+SCRATCH["ints"] = SCRATCH.pop("is")
+for _b in range(8):
+    SCRATCH["b%d" % _b] = ("psum", [128, 512], F)
+SEMAPHORES = ["kl", "xl0", "xl1", "xl2", "xl3", "gi", "v", "s", "p", "sent", "ht", "xt", "mxs", "sls", "landed", "st",
+              "rl0", "rl1", "rl2", "rl3", "rls"]
+FS = {n: 4 * j for j, n in enumerate(["pm", "pk", "pk8", "sc1", "sc2", "rcon", "red", "sdf", "d1", "d2", "dd", "pq", "af", "bf"])}
+FS.update({"jc": 64, "dcon": 80, "lof": 96, "hif": 112, "tc": 128, "ocf": 160})
+IS = {n: 4 * j for j, n in enumerate(["ip", "pm", "pk", "sd", "sdj", "pi", "ai", "bi"])}
+IS.update({"si": 32, "lo": 48, "hi": 64, "oi": 80})
+
+
+def bits(m):
+    return [b for b in range(m.bit_length()) if m >> b & 1]
+
+
+def deal(m, n, w):
+    e = bits(m)
+    return [sum(1 << b for b in e[w * j:w * j + w]) for j in range(n)]
+
+
+def same_chip(topo, a, b):
+    return (topo.host(a), topo.chip(a)) == (topo.host(b), topo.chip(b))
+
+
+def layout(T, topo):
+    mirror, relay, used = {}, {}, []
+    for c in T.cores:
+        mine = [a for a in T.cores if same_chip(topo, a, c) and topo.die(a) == topo.die(c)]
+        far = [a for a in T.cores if not same_chip(topo, a, c) and topo.die(a) == topo.die(c)]
+        mirror[c] = far[mine.index(c)]
+    for c in T.cores:
+        m = mirror[c]
+        if topo.may_write(c, m):
+            continue
+        for z in range(256):
+            if z not in used and topo.mates(z, m) and topo.die(z) == topo.die(c) and topo.may_write(c, z) and topo.may_write(z, m):
+                relay[c] = z
+                used.append(z)
+                break
+    return mirror, relay
+
+
+def rank_program(g, core, T, topo):
+    A, S = AluOpType, T.sem
+    mirror, relay = layout(T, topo)
+    rank = T.rank_of(core)
+    nsent = [0]
+
+    def send(dst, sem, out, src, mask):
+        rid, pid = topo.addr(dst, core)
+        g.remote_dma(out_ap=out, in_ap=src, remote_sem=sem, local_sem=S.sent, pid=pid, routing_id=rid, dma_engine_mask=mask)
+        nsent[0] += len(bits(mask))
+
+    def fused(trs):
+        g.remote_dma_fused([RemoteDMATransfer(
+            dst_ids=[DstId(rid=topo.addr(d, core)[0], pnc=topo.addr(d, core)[1]) for d in ds],
+            dma_engine_mask=mask, remote_sem=sem, srcs=[src], dsts=[out] * len(ds)) for ds, sem, out, src, mask in trs], local_sem=S.sent)
+        nsent[0] += sum(len(bits(t[4])) for t in trs)
+
+    if rank is None:
+        for c in relay:
+            if relay[c] != core:
+                continue
+            n, k, m = len(bits(topo.mask(c, core))), topo.mask(core, mirror[c]), mirror[c]
+            for j, (a, b) in enumerate(PIECES):
+                g.wait_ge(S["rl%d" % j], n)
+                send(m, S.mxs, T.mx[:, a:b], T.mx[:, a:b], k)
+                if j == 1:
+                    g.wait_ge(S.rls, n)
+                    send(m, S.sls, T.slm[:], T.slm[:], k)
+            g.wait_ge(S.sent, nsent[0])
+        return
+
+    def f(name, a=0, b=1):
+        return T.fs[:, FS[name] + a:FS[name] + b]
+
+    def i(name, a=0, b=1):
+        return T.ints[:, IS[name] + a:IS[name] + b]
+
+    me = mirror[core]
+    chip = [c for c in T.cores if same_chip(topo, c, core)]
+    far = [c for c in T.cores if not same_chip(topo, c, core)]
+    ix = chip.index(core)
+    r0 = T.rank_of(chip[0])
+    mrank = T.rank_of(me)
+    direct = core not in relay
+    ports = [c for c in chip if c not in relay]
+    off = topo.mask(core, me if direct else relay[core])
+    onall = topo.mask(core, chip[ix - 1])
+    on = onall & ~off
+    noff = len(bits(off))
+    peers = [chip[(ix + 1 + t) % 8] for t in range(7)]
+    order = peers + [core]
+
+    def tdest(c, there):
+        pc = [a for a in ports if topo.die(a) == topo.die(c)]
+        fd = [a for a in there if topo.die(a) == topo.die(c)]
+        return [d for j, d in enumerate(fd) if pc[j % len(pc)] == c]
+
+    g.sync.dma_start(T.ki[0:16, :], T.key[:]).then_inc(S.kl, 16)
+    for j, q in ((0, g.scalar), (1, g.sync), (2, g.scalar), (3, g.sync)):
+        a, b = PIECES[j]
+        q.dma_start(T.xs[:, a:b], T.x[:, a:b]).then_inc(S["xl%d" % j], 16)
+
+    cnt = {"gi": 0, "v": 0, "s": 0, "p": 0}
+
+    def inc(q, ins):
+        ins.then_inc(S[q], 1)
+        cnt[q] += 1
+        return cnt[q]
+
+    v, pe, sca = g.vector, g.tensor, g.scalar
+
+    def V(ins):
+        return inc("v", ins)
+
+    def P(*a):
+        return inc("p", pe.matmul(*a))
+
+    def vv():
+        v.wait_ge(S.v, cnt["v"])
+
+    def iota(out, pattern, base, cm):
+        return inc("gi", g.iota(out, pattern, base, cm, allow_small_or_imprecise_dtypes=True))
+
+    def half(h):
+        return slice(128 * h, 128 * h + 128)
+
+    iota(i("ip"), [[0, 1]], 0, 1)
+    iota(T.colm[:], [[0, 8], [1, 16]], 0, 0)
+    n_m = iota(T.colk[:], [[1, 8], [0, 16]], 0, 0)
+    n_d = iota(T.dif[:], [[1, 128]], 0, -1)
+    iota(T.colq[:], [[1, 128]], 0, 0)
+    iota(f("jc", 0, 16), [[1, 16]], 0, 16)
+    iota(f("dcon", 0, 16), [[W, 8], [0, 2]], W * r0, 0)
+    n_all = iota(f("ocf", 0, 32), [[0, 16], [16, 2]], 0, 0)
+
+    v.wait_ge(S.gi, n_m)
+    V(v.tensor_scalar(i("pm"), i("ip"), 15, None, A.bitwise_and))
+    V(v.tensor_scalar(i("pk"), i("ip"), 4, None, A.arith_shift_right))
+    V(v.tensor_scalar(T.mr[:], T.colm[:], float(rank), None, A.is_equal))
+    V(v.tensor_scalar(T.ones[:], T.colm[:], 0.0, None, A.is_ge))
+    V(v.tensor_copy(T.colm16[:], T.colm[:]))
+    vv()
+    V(v.tensor_copy(f("pm"), i("pm")))
+    V(v.tensor_copy(f("pk"), i("pk")))
+    vv()
+    V(v.tensor_scalar(T.samem[:], T.colm[:], f("pm"), None, A.is_equal))
+    V(v.tensor_scalar(T.samek[:], T.colk[:], f("pk"), None, A.is_equal))
+    V(v.tensor_scalar(T.ltk[:], T.colk[:], f("pk"), None, A.is_gt))
+    V(v.tensor_scalar(f("pk8"), f("pk"), 8.0, None, A.add))
+    v.wait_ge(S.gi, n_d)
+    V(v.tensor_scalar(T.nle[:], T.dif[:], 0.0, -1.0, A.is_le, A.mult))
+    vv()
+    V(v.tensor_tensor(T.samekr[:], T.samek[:], T.mr[:], A.mult))
+    V(v.tensor_tensor(T.ltkr[:], T.ltk[:], T.mr[:], A.mult))
+    V(v.tensor_tensor(T.bm[:], T.samek[:], T.nle[:], A.mult))
+
+    v.wait_ge(S.kl, 16)
+    n = V(v.tensor_copy(T.k16[0:16, :], T.ki[0:16, :]))
+    pe.wait_ge(S.v, n)
+    n = P(T.b0[:, 0:128], T.samem[0:16, :], T.k16[0:16, :], True, True)
+    v.wait_ge(S.p, n)
+    V(v.tensor_scalar(T.oh[:, 0:128], T.b0[:, 0:128], f("pk"), None, A.is_equal))
+    V(v.tensor_scalar(T.oh[:, 128:256], T.b0[:, 0:128], f("pk8"), None, A.is_equal))
+    vv()
+    V(v.tensor_tensor_scan(T.sc[:, 0:128], T.ones[:], T.oh[:, 0:128], 0.0, A.mult, A.add))
+    n = V(v.tensor_tensor_scan(T.sc[:, 128:256], T.ones[:], T.oh[:, 128:256], 0.0, A.mult, A.add))
+    pe.wait_ge(S.v, n)
+    tot = T.sc[:, 127:256:128]
+    P(T.b1[:, 0:2], T.samekr[:], tot, True, True)
+    P(T.b1[:, 2:4], T.ltkr[:], tot, True, False)
+    n_h = P(T.b1[:, 3:4], T.mr[:], T.sc[:, 127:128], False, True)
+    P(T.b3[:, 32:34], T.ltk[:], tot, True, False)
+    P(T.b3[:, 33:34], T.ones[:], T.sc[:, 127:128], False, True)
+    for h in range(2):
+        P(T.b2[:, half(h)], T.samek[:], T.sc[:, half(h)], True, False)
+        n_w = P(T.b2[:, half(h)], T.bm[:], T.oh[:, half(h)], False, True)
+    v.wait_ge(S.p, n_h)
+    n_hist = V(v.tensor_copy(T.lt[:, 4 * rank:4 * rank + 4], T.b1[:, 0:4]))
+
+    v.wait_ge(S.p, n_w)
+    for h in range(2):
+        V(v.tensor_scalar(T.wb[:, half(h)], T.b2[:, half(h)], T.b3[:, 32 + h:33 + h], None, A.add))
+    vv()
+    n = V(v.tensor_tensor(T.ow[:], T.wb[:], T.oh[:], A.mult))
+    pe.wait_ge(S.v, n)
+    P(T.b3[:, 0:16], T.ow[:, 0:128], T.samem[:, 0:16], True, False)
+    n = P(T.b3[:, 0:16], T.ow[:, 128:256], T.samem[:, 0:16], False, True)
+    v.wait_ge(S.gi, n_all)
+    V(v.tensor_copy(T.colq16[:], T.colq[:]))
+    V(v.memset(T.sl[:, 128:160], 0.0))
+    V(v.memset(T.slx[:, 128:160], 0.0))
+    v.wait_ge(S.p, n)
+    V(v.tensor_copy(i("si", 0, 16), T.b3[:, 0:16]))
+    vv()
+    V(v.tensor_scalar(i("lo", 0, 16), i("si", 0, 16), 15, None, A.bitwise_and))
+    V(v.tensor_scalar(i("hi", 0, 16), i("si", 0, 16), 4, None, A.arith_shift_right))
+    vv()
+    V(v.tensor_copy(f("lof", 0, 16), i("lo", 0, 16)))
+    V(v.tensor_copy(f("hif", 0, 16), i("hi", 0, 16)))
+    vv()
+    for m in range(16):
+        V(v.tensor_scalar(T.lh[:, half(m)], T.colm16[:], f("lof", m, m + 1), f("jc", m, m + 1), A.is_equal, A.mult))
+        n = V(v.tensor_scalar(T.rh[:, half(m)], T.colq16[:], f("hif", m, m + 1), None, A.is_equal))
+        pe.wait_ge(S.v, n)
+        n = P(T.b4[:, 0:128], T.lh[:, half(m)], T.rh[:, half(m)], m == 0, m == 15)
+    v.wait_ge(S.p, n)
+    n_slu = V(v.tensor_copy(T.slu[:], T.b4[:, 0:128]))
+    V(v.tensor_copy(T.sl[:, 0:128], T.b4[:, 0:128]))
+
+    V(v.tensor_scalar(T.um[:], T.dif[:], 0.0, None, A.is_gt))
+    V(v.tensor_scalar(T.ident[:], T.dif[:], 0.0, None, A.is_equal))
+    V(v.tensor_scalar(f("sc1"), f("pm"), float(rank), 0.0625, A.is_equal, A.mult))
+    V(v.tensor_scalar(f("sc2"), f("pm"), float(mrank), 0.0625, A.is_equal, A.mult))
+    V(v.tensor_scalar(T.oc[:], f("ocf", 0, 32), f("pm"), -0.46875, A.add, A.add))
+    V(v.tensor_scalar(T.ee[:, 0:128], T.dif[:], 0.0, None, A.is_equal))
+    V(v.tensor_scalar(T.ee[:, 128:256], T.dif[:], 1.0, None, A.is_equal))
+    V(v.tensor_scalar(T.fm[:], T.dif[:], -127.0, -1.0, A.is_equal, A.mult))
+    V(v.tensor_scalar(T.posc[:], T.colq[:], 16.0, f("pm"), A.mult, A.add))
+    V(v.tensor_scalar(f("rcon"), f("pm"), float(SLOT), float(W * rank), A.mult, A.add))
+    vv()
+    V(v.tensor_tensor(T.em[:], T.ee[:, 0:128], T.ee[:, 128:256], A.subtract))
+    V(v.tensor_scalar(T.selo[:], T.ones[:], f("sc1"), None, A.mult))
+    V(v.tensor_scalar(T.selm[:], T.ones[:], f("sc2"), None, A.mult))
+
+    v.wait_ge(S.ht, 7 * len(bits(on)))
+    v.wait_ge(S.xt, noff)
+    vv()
+    for j in range(4):
+        V(v.tensor_reduce(f("red", j, j + 1), T.lt[:, j:64:4], AxisListType.X, A.add))
+    vv()
+    n = V(v.tensor_copy(T.c16[:, 0:2], f("red", 0, 2)))
+    pe.wait_ge(S.v, n)
+    P(T.b5[:, 0:2], T.um[:], T.c16[:, 0:2], True, False)
+    n = P(T.b5[:, 1:2], T.ones[:], T.c16[:, 0:1], False, True)
+    v.wait_ge(S.p, n)
+    for h in range(2):
+        V(v.tensor_scalar(f("tc", 16 * h, 16 * h + 16), f("dcon", 0, 16), T.b5[:, h:h + 1], 0.0, A.subtract, A.max))
+    vv()
+    for h in range(2):
+        n = V(v.tensor_scalar(T.cl[:, 16 * h:16 * h + 16], f("tc", 16 * h, 16 * h + 16), f("red", h, h + 1), None, A.min))
+    pe.wait_ge(S.v, n)
+    for q, sel in ((0, T.selo), (16, T.selm)):
+        P(T.b6[:, q:q + 16], T.ident[:], T.oc[:, 0:16], True, False)
+        P(T.b6[:, q:q + 16], sel[:], T.cl[:, 0:16], False, False)
+        n = P(T.b6[:, q:q + 16], sel[:], T.cl[:, 16:32], False, True)
+    P(T.b7[:, 0:1], T.samem[:], T.cl[:, 2 * ix:2 * ix + 1], True, False)
+    n_srd = P(T.b7[:, 0:1], T.samem[:], T.cl[:, 16 + 2 * ix:17 + 2 * ix], False, True)
+    v.wait_ge(S.p, n)
+    V(v.tensor_copy(i("oi", 0, 32), T.b6[:, 0:32]))
+    vv()
+    V(v.tensor_copy(T.ou[:], i("oi", 0, 32)))
+    vv()
+    n_lown = V(v.tensor_copy(T.lown[:], T.sl[:, 0:160].indirect(T.ou[:, 0:16])))
+    v.wait_ge(S.sls, noff)
+    V(v.tensor_copy(T.slx[:, 0:128], T.slm[:]))
+    vv()
+    n_lmir = V(v.tensor_copy(T.lmir[:], T.slx[:, 0:160].indirect(T.ou[:, 16:32])))
+
+    for q in (v, sca):
+        for j in range(4):
+            q.wait_ge(S["xl%d" % j], 16)
+    done = {}
+    sca.wait_ge(S.v, n_lown)
+    nmx = noff * (3 if direct else 4)
+    for which, src, lst, buf, rk in (("o", T.xs, T.lown, T.so, rank), ("m", T.mx, T.lmir, T.sm, mrank)):
+        if which == "m":
+            sca.wait_ge(S.v, n_lmir)
+            vv()
+            for q in (v, sca):
+                q.wait_ge(S.mxs, nmx)
+        for t in range(8):
+            d = chip.index(order[t])
+            out = T.land[:, SLOT * rk:SLOT * rk + SLOT] if t == 7 else buf[:, SLOT * t:SLOT * t + SLOT]
+            win = src[:, 0:W].indirect(lst[:, 32 * d:32 * d + 17])
+            if t % 2:
+                V(v.tensor_copy(out, win))
+            else:
+                inc("s", sca.activation(out, win, ActivationFunctionType.Copy))
+            done[which, t] = (cnt["v"], cnt["s"])
+
+    v.wait_ge(S.p, n_srd)
+    V(v.tensor_copy(i("sd"), T.b7[:, 0:1]))
+    V(v.tensor_tensor(f("d1", 0, 2), f("red", 2, 4), T.b5[:, 0:2], A.subtract))
+    V(v.tensor_scalar(f("pq", 0, 2), T.b5[:, 0:2], float(-W * rank), None, A.add))
+    vv()
+    V(v.tensor_scalar(i("sdj"), i("sd"), 0xFFF0, None, A.bitwise_and))
+    V(v.tensor_copy(i("pi", 0, 2), f("pq", 0, 2)))
+    vv()
+    V(v.tensor_copy(f("sdf"), i("sdj")))
+    V(v.tensor_scalar(i("ai", 0, 2), i("pi", 0, 2), 4, None, A.arith_shift_right))
+    V(v.tensor_scalar(i("bi", 0, 2), i("pi", 0, 2), 15, None, A.bitwise_and))
+    vv()
+    n = V(v.tensor_scalar(f("d2", 0, 2), f("d1", 0, 2), f("sdf"), f("rcon"), A.subtract, A.add))
+    V(v.tensor_copy(f("af", 0, 2), i("ai", 0, 2)))
+    V(v.tensor_copy(f("bf", 0, 2), i("bi", 0, 2)))
+    pe.wait_ge(S.v, n)
+    P(T.b7[:, 8:10], T.em[:], f("d2", 0, 2), True, False)
+    n = P(T.b7[:, 9:10], T.fm[:], f("d2", 0, 1), False, True)
+    vv()
+    for h in range(2):
+        V(v.tensor_scalar(T.rl[:, half(h)], T.colq[:], f("af", h, h + 1), None, A.is_gt))
+        V(v.tensor_scalar(T.rl[:, half(2 + h)], T.colq[:], f("af", h, h + 1), None, A.is_equal))
+    v.wait_ge(S.p, n)
+    V(v.tensor_copy(f("dd", 0, 2), T.b7[:, 8:10]))
+    vv()
+    for h in range(2):
+        V(v.tensor_scalar(T.ll[:, half(h)], T.colq[:], 0.0, f("dd", h, h + 1), A.is_ge, A.mult))
+        n = V(v.tensor_scalar(T.ll[:, half(2 + h)], T.colm[:], f("bf", h, h + 1), f("dd", h, h + 1), A.is_ge, A.mult))
+    pe.wait_ge(S.v, n)
+    for h in range(4):
+        n = P(T.b0[:, 0:128], T.ll[:, half(h)], T.rl[:, half(h)], h == 0, h == 3)
+    v.wait_ge(S.p, n)
+    V(v.tensor_tensor(T.fi[:], T.b0[:, 0:128], T.posc[:], A.add))
+    vv()
+    n_fu = V(v.tensor_copy(T.fu[:], T.fi[:]))
+
+    vv()
+    v.wait_ge(S.landed, 7 * (2 + 4))
+    sca.wait_ge(S.v, n_fu)
+    sca.wait_ge(S.landed, 7 * (2 + 4))
+    ready = []
+    for c in range(4):
+        win = T.land[:, 0:16 * SLOT].indirect(T.fu[:, 32 * c:32 * c + 32])
+        out = T.ys[:, 512 * c:512 * c + 512]
+        if c % 2:
+            ready.append(("s", inc("s", sca.activation(out, win, ActivationFunctionType.Copy))))
+        else:
+            ready.append(("v", V(v.tensor_copy(out, win))))
+    for c, (q, n) in enumerate(ready):
+        g.sync.wait_ge(S[q], n)
+        g.sync.dma_start(T.y[:, 512 * c:512 * c + 512], T.ys[:, 512 * c:512 * c + 512]).then_inc(S.st, 16)
+
+    def xsend(j, a, b):
+        if direct:
+            send(me, S.mxs, T.mx[:, a:b], T.xs[:, a:b], off)
+        else:
+            send(relay[core], S["rl%d" % j], T.mx[:, a:b], T.xs[:, a:b], off)
+
+    g.wait_ge(S.xl0, 16)
+    xsend(0, 0, 512)
+    g.wait_ge(S.v, n_hist)
+    mine = T.lt[:, 4 * rank:4 * rank + 4]
+    for grp in ([c for c in peers if c in ports], [c for c in peers if c not in ports]):
+        fused([(grp, S.ht, mine, mine, on)])
+    g.wait_ge(S.xl1, 16)
+    xsend(1, 512, 1024)
+    if direct:
+        g.wait_ge(S.ht, 7 * len(bits(on)))
+        blk = T.lt[:, 4 * r0:4 * r0 + 32]
+        fused([(tdest(core, far), S.xt, blk, blk, off)])
+    g.wait_ge(S.v, n_slu)
+    send(me if direct else relay[core], S.sls if direct else S.rls, T.slm[:], T.slu[:], off)
+    g.wait_ge(S.xl2, 16)
+    g.wait_ge(S.xl3, 16)
+    if direct:
+        xsend(2, 1024, 2048)
+    else:
+        xsend(2, 1024, 1536)
+        xsend(3, 1536, 2048)
+    for which, buf, rk, eng, w in (("o", T.so, rank, on, 2), ("m", T.sm, mrank, onall, 4)):
+        ms = deal(eng, 4, w)
+        out = T.land[:, SLOT * rk:SLOT * rk + SLOT]
+        for ts in ((0, 1, 2, 3), (4, 5, 6)):
+            nv, ns = done[which, ts[-1]]
+            g.wait_ge(S.v, nv)
+            g.wait_ge(S.s, ns)
+            fused([([order[t]], S.landed, out, buf[:, SLOT * t:SLOT * t + SLOT], ms[j]) for j, t in enumerate(ts)])
+    g.wait_ge(S.sent, nsent[0])
+    g.sync.wait_ge(S.st, 64)
+    for q in ("gi", "v", "s", "p"):
+        g.sync.wait_ge(S[q], cnt[q])

@@ -4,46 +4,47 @@ from concourse.mybir import dt, AluOpType, AxisListType, ActivationFunctionType
 
 W = 2048
 SLOT = 272
+PAIR = 2 * SLOT
+BIG = 12582912.0
 PIECES = [(0, 512), (512, 1024), (1024, 1536), (1536, 2048)]
 F, H, I, U, B = "float32", "float16", "int32", "uint16", "bfloat16"
 SCRATCH = {
     "xs": ("sbuf", [128, W], B), "mx": ("sbuf", [128, W], B), "ys": ("sbuf", [128, W], B),
-    "so": ("sbuf", [128, 8 * SLOT], B), "sm": ("sbuf", [128, 8 * SLOT], B), "land": ("sbuf", [128, 16 * SLOT], B),
+    "so": ("sbuf", [128, 7 * PAIR], B), "land": ("sbuf", [128, 8 * PAIR], B),
     "ki": ("sbuf", [128, 128], I), "k16": ("sbuf", [128, 128], H),
-    "fs": ("sbuf", [128, 256], F), "is": ("sbuf", [128, 128], I),
+    "fs": ("sbuf", [128, 384], F), "ints": ("sbuf", [128, 16], I),
     "colm": ("sbuf", [128, 128], F), "colk": ("sbuf", [128, 128], F), "colq": ("sbuf", [128, 128], F), "dif": ("sbuf", [128, 128], F),
-    "oc": ("sbuf", [128, 32], H),
-    "colm16": ("sbuf", [128, 128], H), "colq16": ("sbuf", [128, 128], H),
-    "ones": ("sbuf", [128, 128], H), "mr": ("sbuf", [128, 128], H), "samem": ("sbuf", [128, 128], H), "samek": ("sbuf", [128, 128], H),
-    "ltk": ("sbuf", [128, 128], H), "nle": ("sbuf", [128, 128], H), "bm": ("sbuf", [128, 128], H),
+    "oc": ("sbuf", [128, 32], H), "cm": ("sbuf", [128, 16], H),
+    "mrow": ("sbuf", [128, 128], H), "colq16": ("sbuf", [128, 128], H),
+    "ones": ("sbuf", [128, 128], H), "mr": ("sbuf", [128, 128], H), "samem": ("sbuf", [128, 128], H), "samem16": ("sbuf", [128, 128], H),
+    "samek": ("sbuf", [128, 128], H), "ltk": ("sbuf", [128, 128], H), "nle": ("sbuf", [128, 128], H), "bm": ("sbuf", [128, 128], H),
     "samekr": ("sbuf", [128, 128], H), "ltkr": ("sbuf", [128, 128], H), "um": ("sbuf", [128, 128], H), "ident": ("sbuf", [128, 128], H),
     "selo": ("sbuf", [128, 128], H), "selm": ("sbuf", [128, 128], H),
-    "ee": ("sbuf", [128, 256], F), "em": ("sbuf", [128, 128], F), "fm": ("sbuf", [128, 128], F), "posc": ("sbuf", [128, 128], F),
+    "ee": ("sbuf", [128, 256], F), "e0": ("sbuf", [128, 128], F), "e1": ("sbuf", [128, 128], F), "fm": ("sbuf", [128, 128], F),
+    "posc": ("sbuf", [128, 128], H),
     "oh": ("sbuf", [128, 256], H), "sc": ("sbuf", [128, 256], H), "wb": ("sbuf", [128, 256], H), "ow": ("sbuf", [128, 256], H),
     "lh": ("sbuf", [128, 2048], H), "rh": ("sbuf", [128, 2048], H),
-    "sl": ("sbuf", [128, 160], F), "slx": ("sbuf", [128, 160], F), "slu": ("sbuf", [128, 128], U), "slm": ("sbuf", [128, 128], U),
-    "lt": ("sbuf", [128, 64], F), "c16": ("sbuf", [128, 4], H), "cl": ("sbuf", [128, 32], H), "ou": ("sbuf", [128, 32], U),
+    "sl": ("sbuf", [128, 160], F), "slx": ("sbuf", [128, 160], F),
+    "lt": ("sbuf", [128, 64], F), "cc": ("sbuf", [128, 32], H), "cl": ("sbuf", [128, 32], H), "ou": ("sbuf", [128, 32], U),
     "lown": ("sbuf", [128, 256], U), "lmir": ("sbuf", [128, 256], U),
-    "rl": ("sbuf", [128, 512], F), "ll": ("sbuf", [128, 512], F), "fi": ("sbuf", [128, 128], F), "fu": ("sbuf", [128, 128], U),
+    "rl": ("sbuf", [128, 512], H), "ll": ("sbuf", [128, 1024], H), "fu": ("sbuf", [128, 128], U),
 }
-SCRATCH["ints"] = SCRATCH.pop("is")
 for _b in range(8):
     SCRATCH["b%d" % _b] = ("psum", [128, 512], F)
 SEMAPHORES = ["kl", "xl0", "xl1", "xl2", "xl3", "gi", "v", "s", "p", "sent", "ht", "xt", "mxs", "sls", "landed", "st",
               "rl0", "rl1", "rl2", "rl3", "rls"]
-FS = {n: 4 * j for j, n in enumerate(["pm", "pk", "pk8", "sc1", "sc2", "rcon", "red", "sdf", "d1", "d2", "dd", "pq", "af", "bf"])}
-FS.update({"jc": 64, "dcon": 80, "lof": 96, "hif": 112, "tc": 128, "ocf": 160})
-IS = {n: 4 * j for j, n in enumerate(["ip", "pm", "pk", "sd", "sdj", "pi", "ai", "bi"])}
-IS.update({"si": 32, "lo": 48, "hi": 64, "oi": 80})
+FS = {n: 4 * j for j, n in enumerate(["pm", "pk", "pk8", "sc1", "sc2", "rca", "rcb", "rcon", "red", "z", "d1", "ac", "an", "bz", "s1", "s2",
+                                      "e", "dd", "nd", "dc", "h0", "h1", "hh", "lw"])}
+FS.update({"jc": 128, "dcon": 144, "lof": 160, "hif": 176, "tc": 192, "ocf": 224})
+IS = {"ip": 0, "pm": 4, "pk": 8}
 
 
 def bits(m):
     return [b for b in range(m.bit_length()) if m >> b & 1]
 
 
-def deal(m, n, w):
-    e = bits(m)
-    return [sum(1 << b for b in e[w * j:w * j + w]) for j in range(n)]
+def unbits(e):
+    return sum(1 << b for b in e)
 
 
 def same_chip(topo, a, b):
@@ -68,8 +69,20 @@ def layout(T, topo):
     return mirror, relay
 
 
+def exchange(T, topo, c):
+    here = [a for a in T.cores if same_chip(topo, a, c)]
+    own = [a for a in here if topo.die(a) == topo.die(c)]
+    oth = [a for a in here if topo.die(a) != topo.die(c)]
+    k, n = own.index(c), len(own)
+    own = [own[(k + 1 + t) % n] for t in range(n - 1)]
+    oth = [oth[(k + t) % n] for t in range(n)]
+    e = bits(topo.mask(c, oth[0]))
+    calls = [[(oth[t], unbits(e[0::2])), (own[t], unbits(e[1::2]))] for t in range(n - 1)]
+    return calls + [[(oth[n - 1], unbits(e))]]
+
+
 def rank_program(g, core, T, topo):
-    A, S = AluOpType, T.sem
+    A, S, AF = AluOpType, T.sem, ActivationFunctionType
     mirror, relay = layout(T, topo)
     rank = T.rank_of(core)
     nsent = [0]
@@ -91,19 +104,19 @@ def rank_program(g, core, T, topo):
                 continue
             n, k, m = len(bits(topo.mask(c, core))), topo.mask(core, mirror[c]), mirror[c]
             for j, (a, b) in enumerate(PIECES):
+                if j == 3:
+                    g.wait_ge(S.rls, n)
+                    send(m, S.sls, T.slx[:, 0:128], T.slx[:, 0:128], k)
                 g.wait_ge(S["rl%d" % j], n)
                 send(m, S.mxs, T.mx[:, a:b], T.mx[:, a:b], k)
-                if j == 1:
-                    g.wait_ge(S.rls, n)
-                    send(m, S.sls, T.slm[:], T.slm[:], k)
             g.wait_ge(S.sent, nsent[0])
         return
 
     def f(name, a=0, b=1):
         return T.fs[:, FS[name] + a:FS[name] + b]
 
-    def i(name, a=0, b=1):
-        return T.ints[:, IS[name] + a:IS[name] + b]
+    def i(name):
+        return T.ints[:, IS[name]:IS[name] + 1]
 
     me = mirror[core]
     chip = [c for c in T.cores if same_chip(topo, c, core)]
@@ -114,11 +127,15 @@ def rank_program(g, core, T, topo):
     direct = core not in relay
     ports = [c for c in chip if c not in relay]
     off = topo.mask(core, me if direct else relay[core])
-    onall = topo.mask(core, chip[ix - 1])
-    on = onall & ~off
+    on = topo.mask(core, chip[ix - 1]) & ~off
     noff = len(bits(off))
     peers = [chip[(ix + 1 + t) % 8] for t in range(7)]
-    order = peers + [core]
+    calls = exchange(T, topo, core)
+    order = [d for c in calls for d, m in c] + [core]
+    nland = sum(len(bits(m)) for p in peers for c in exchange(T, topo, p) for d, m in c if d == core)
+    place = [PAIR * chip.index(c) if c in chip else PAIR * chip.index(mirror[c]) + SLOT for c in T.cores]
+    step = place[8] - place[0] - 8 * PAIR
+    assert place == [place[0] + PAIR * r + (step if r >= 8 else 0) for r in range(16)]
 
     def tdest(c, there):
         pc = [a for a in ports if topo.die(a) == topo.die(c)]
@@ -145,8 +162,14 @@ def rank_program(g, core, T, topo):
     def P(*a):
         return inc("p", pe.matmul(*a))
 
+    def C(out, in_, func=AF.Identity, bias=0.0, scale=1.0):
+        return inc("s", sca.activation(out, in_, func, bias=bias, scale=scale))
+
     def vv():
         v.wait_ge(S.v, cnt["v"])
+
+    def ss():
+        sca.wait_ge(S.s, cnt["s"])
 
     def iota(out, pattern, base, cm):
         return inc("gi", g.iota(out, pattern, base, cm, allow_small_or_imprecise_dtypes=True))
@@ -163,12 +186,19 @@ def rank_program(g, core, T, topo):
     iota(f("dcon", 0, 16), [[W, 8], [0, 2]], W * r0, 0)
     n_all = iota(f("ocf", 0, 32), [[0, 16], [16, 2]], 0, 0)
 
+    sca.wait_ge(S.gi, n_d)
+    C(T.ee[:, 0:128], T.dif[:], AF.Abs)
+    C(T.ee[:, 128:256], T.dif[:], AF.Abs, bias=-1.0)
+    C(T.fm[:], T.dif[:], AF.Relu, bias=-126.0, scale=-1.0)
+    ss()
+    C(T.e0[:], T.ee[:, 0:128], AF.Relu, bias=1.0, scale=-1.0)
+    C(T.e1[:], T.ee[:, 128:256], AF.Relu, bias=1.0, scale=-1.0)
+
     v.wait_ge(S.gi, n_m)
     V(v.tensor_scalar(i("pm"), i("ip"), 15, None, A.bitwise_and))
     V(v.tensor_scalar(i("pk"), i("ip"), 4, None, A.arith_shift_right))
     V(v.tensor_scalar(T.mr[:], T.colm[:], float(rank), None, A.is_equal))
     V(v.tensor_scalar(T.ones[:], T.colm[:], 0.0, None, A.is_ge))
-    V(v.tensor_copy(T.colm16[:], T.colm[:]))
     vv()
     V(v.tensor_copy(f("pm"), i("pm")))
     V(v.tensor_copy(f("pk"), i("pk")))
@@ -210,150 +240,159 @@ def rank_program(g, core, T, topo):
     v.wait_ge(S.p, n_w)
     for h in range(2):
         V(v.tensor_scalar(T.wb[:, half(h)], T.b2[:, half(h)], T.b3[:, 32 + h:33 + h], None, A.add))
+    V(v.tensor_scalar(T.samem16[:], T.samem[:], 0.0625, None, A.mult))
+    V(v.tensor_scalar(T.cm[:], T.colm[:, 0:16], 0.0, -15.0 / 4096, A.mult, A.add))
     vv()
     n = V(v.tensor_tensor(T.ow[:], T.wb[:], T.oh[:], A.mult))
     pe.wait_ge(S.v, n)
-    P(T.b3[:, 0:16], T.ow[:, 0:128], T.samem[:, 0:16], True, False)
-    n = P(T.b3[:, 0:16], T.ow[:, 128:256], T.samem[:, 0:16], False, True)
+    P(T.b3[:, 0:16], T.ones[:], T.cm[:], True, False)
+    P(T.b3[:, 0:16], T.ow[:, 0:128], T.samem16[:, 0:16], False, False)
+    n = P(T.b3[:, 0:16], T.ow[:, 128:256], T.samem16[:, 0:16], False, True)
     v.wait_ge(S.gi, n_all)
     V(v.tensor_copy(T.colq16[:], T.colq[:]))
+    V(v.tensor_scalar(T.mrow[:], T.colm[:], 0.0625, -0.46875, A.mult, A.add))
     V(v.memset(T.sl[:, 128:160], 0.0))
     V(v.memset(T.slx[:, 128:160], 0.0))
     v.wait_ge(S.p, n)
-    V(v.tensor_copy(i("si", 0, 16), T.b3[:, 0:16]))
+    V(v.tensor_scalar(f("hif", 0, 16), T.b3[:, 0:16], BIG, -BIG, A.add, A.add))
     vv()
-    V(v.tensor_scalar(i("lo", 0, 16), i("si", 0, 16), 15, None, A.bitwise_and))
-    V(v.tensor_scalar(i("hi", 0, 16), i("si", 0, 16), 4, None, A.arith_shift_right))
-    vv()
-    V(v.tensor_copy(f("lof", 0, 16), i("lo", 0, 16)))
-    V(v.tensor_copy(f("hif", 0, 16), i("hi", 0, 16)))
-    vv()
+    V(v.tensor_tensor(f("lof", 0, 16), T.b3[:, 0:16], f("hif", 0, 16), A.subtract))
     for m in range(16):
-        V(v.tensor_scalar(T.lh[:, half(m)], T.colm16[:], f("lof", m, m + 1), f("jc", m, m + 1), A.is_equal, A.mult))
-        n = V(v.tensor_scalar(T.rh[:, half(m)], T.colq16[:], f("hif", m, m + 1), None, A.is_equal))
+        V(v.tensor_scalar(T.rh[:, half(m)], T.colq16[:], f("hif", m, m + 1), None, A.is_equal))
+        if m == 0:
+            vv()
+        n = V(v.tensor_scalar(T.lh[:, half(m)], T.mrow[:], f("lof", m, m + 1), f("jc", m, m + 1), A.is_equal, A.mult))
         pe.wait_ge(S.v, n)
         n = P(T.b4[:, 0:128], T.lh[:, half(m)], T.rh[:, half(m)], m == 0, m == 15)
-    v.wait_ge(S.p, n)
-    n_slu = V(v.tensor_copy(T.slu[:], T.b4[:, 0:128]))
-    V(v.tensor_copy(T.sl[:, 0:128], T.b4[:, 0:128]))
+    sca.wait_ge(S.p, n)
+    n_sl = C(T.sl[:, 0:128], T.b4[:, 0:128])
 
     V(v.tensor_scalar(T.um[:], T.dif[:], 0.0, None, A.is_gt))
     V(v.tensor_scalar(T.ident[:], T.dif[:], 0.0, None, A.is_equal))
     V(v.tensor_scalar(f("sc1"), f("pm"), float(rank), 0.0625, A.is_equal, A.mult))
     V(v.tensor_scalar(f("sc2"), f("pm"), float(mrank), 0.0625, A.is_equal, A.mult))
     V(v.tensor_scalar(T.oc[:], f("ocf", 0, 32), f("pm"), -0.46875, A.add, A.add))
-    V(v.tensor_scalar(T.ee[:, 0:128], T.dif[:], 0.0, None, A.is_equal))
-    V(v.tensor_scalar(T.ee[:, 128:256], T.dif[:], 1.0, None, A.is_equal))
-    V(v.tensor_scalar(T.fm[:], T.dif[:], -127.0, -1.0, A.is_equal, A.mult))
-    V(v.tensor_scalar(T.posc[:], T.colq[:], 16.0, f("pm"), A.mult, A.add))
-    V(v.tensor_scalar(f("rcon"), f("pm"), float(SLOT), float(W * rank), A.mult, A.add))
+    V(v.tensor_scalar(f("rca"), f("pm"), 8.0, float(step), A.is_ge, A.mult))
+    V(v.tensor_scalar(f("rcb"), f("pm"), float(PAIR), float(place[0] + W * rank), A.mult, A.add))
     vv()
-    V(v.tensor_tensor(T.em[:], T.ee[:, 0:128], T.ee[:, 128:256], A.subtract))
     V(v.tensor_scalar(T.selo[:], T.ones[:], f("sc1"), None, A.mult))
     V(v.tensor_scalar(T.selm[:], T.ones[:], f("sc2"), None, A.mult))
+    V(v.tensor_tensor(f("rcon"), f("rca"), f("rcb"), A.add))
+    V(v.tensor_scalar(T.posc[:], T.colq[:], 16.0, f("pm"), A.mult, A.add))
 
     v.wait_ge(S.ht, 7 * len(bits(on)))
     v.wait_ge(S.xt, noff)
     vv()
+    for j in range(2):
+        n = V(v.tensor_tensor_scan(T.cc[:, 16 * j:16 * j + 16], T.ones[:, 0:16], T.lt[:, j:64:4], 0.0, A.mult, A.add))
     for j in range(4):
-        V(v.tensor_reduce(f("red", j, j + 1), T.lt[:, j:64:4], AxisListType.X, A.add))
-    vv()
-    n = V(v.tensor_copy(T.c16[:, 0:2], f("red", 0, 2)))
+        n_red = V(v.tensor_reduce(f("red", j, j + 1), T.lt[:, j:64:4], AxisListType.X, A.add))
     pe.wait_ge(S.v, n)
-    P(T.b5[:, 0:2], T.um[:], T.c16[:, 0:2], True, False)
-    n = P(T.b5[:, 1:2], T.ones[:], T.c16[:, 0:1], False, True)
-    v.wait_ge(S.p, n)
+    for bk, c in ((T.b5, 0), (T.b1, 8)):
+        P(bk[:, c:c + 2], T.um[:], T.cc[:, 15:32:16], True, False)
+        n_p = P(bk[:, c + 1:c + 2], T.ones[:], T.cc[:, 15:16], False, True)
+        if c == 0:
+            v.wait_ge(S.p, n_p)
     for h in range(2):
         V(v.tensor_scalar(f("tc", 16 * h, 16 * h + 16), f("dcon", 0, 16), T.b5[:, h:h + 1], 0.0, A.subtract, A.max))
     vv()
     for h in range(2):
         n = V(v.tensor_scalar(T.cl[:, 16 * h:16 * h + 16], f("tc", 16 * h, 16 * h + 16), f("red", h, h + 1), None, A.min))
     pe.wait_ge(S.v, n)
-    for q, sel in ((0, T.selo), (16, T.selm)):
-        P(T.b6[:, q:q + 16], T.ident[:], T.oc[:, 0:16], True, False)
-        P(T.b6[:, q:q + 16], sel[:], T.cl[:, 0:16], False, False)
-        n = P(T.b6[:, q:q + 16], sel[:], T.cl[:, 16:32], False, True)
-    P(T.b7[:, 0:1], T.samem[:], T.cl[:, 2 * ix:2 * ix + 1], True, False)
-    n_srd = P(T.b7[:, 0:1], T.samem[:], T.cl[:, 16 + 2 * ix:17 + 2 * ix], False, True)
-    v.wait_ge(S.p, n)
-    V(v.tensor_copy(i("oi", 0, 32), T.b6[:, 0:32]))
-    vv()
-    V(v.tensor_copy(T.ou[:], i("oi", 0, 32)))
-    vv()
+    ns = []
+    for bk, sel in ((T.b6, T.selo), (T.b2, T.selm)):
+        P(bk[:, 0:16], T.ident[:], T.oc[:, 0:16], True, False)
+        P(bk[:, 0:16], sel[:], T.cl[:, 0:16], False, False)
+        ns.append(P(bk[:, 0:16], sel[:], T.cl[:, 16:32], False, True))
+    P(T.b7[:, 0:1], T.ones[:], T.cm[:, 0:1], True, False)
+    P(T.b7[:, 0:1], T.samem16[:], T.cl[:, 2 * ix:2 * ix + 1], False, False)
+    n_srd = P(T.b7[:, 0:1], T.samem16[:], T.cl[:, 16 + 2 * ix:17 + 2 * ix], False, True)
+    v.wait_ge(S.p, ns[0])
+    n1 = V(v.tensor_scalar(T.ou[:, 0:16], T.b6[:, 0:16], BIG, -BIG, A.add, A.add))
+    v.wait_ge(S.p, ns[1])
+    n2 = V(v.tensor_scalar(T.ou[:, 16:32], T.b2[:, 0:16], BIG, -BIG, A.add, A.add))
+    v.wait_ge(S.s, n_sl)
+    v.wait_ge(S.v, n2)
     n_lown = V(v.tensor_copy(T.lown[:], T.sl[:, 0:160].indirect(T.ou[:, 0:16])))
     v.wait_ge(S.sls, noff)
-    V(v.tensor_copy(T.slx[:, 0:128], T.slm[:]))
-    vv()
     n_lmir = V(v.tensor_copy(T.lmir[:], T.slx[:, 0:160].indirect(T.ou[:, 16:32])))
 
-    for q in (v, sca):
-        for j in range(4):
-            q.wait_ge(S["xl%d" % j], 16)
-    done = {}
+    sca.wait_ge(S.p, n_p)
+    C(f("z", 0, 2), T.b1[:, 8:10], bias=-0.46875 - W * rank / 16.0, scale=0.0625)
+    sca.wait_ge(S.v, n_red)
+    for h in range(2):
+        C(f("d1", h, h + 1), T.b1[:, 8 + h:9 + h], bias=f("red", 2 + h, 3 + h), scale=-1.0)
+    ss()
+    C(f("ac", 0, 2), f("z", 0, 2), bias=BIG)
+    ss()
+    C(f("an", 0, 2), f("ac", 0, 2), bias=-BIG)
+    sca.wait_ge(S.p, n_srd)
+    C(f("s1"), T.b7[:, 0:1], bias=BIG)
+    ss()
+    for h in range(2):
+        C(f("bz", h, h + 1), f("an", h, h + 1), bias=f("z", h, h + 1), scale=-1.0)
+    C(f("s2"), f("s1"), bias=-BIG)
+    ss()
+    C(f("e"), f("s2"), bias=f("rcon"), scale=-16.0)
+    ss()
+    C(f("dd", 0, 2), f("d1", 0, 2), bias=f("e"))
+    ss()
+    n = C(f("nd", 0, 2), f("dd", 0, 2), scale=-1.0)
+    pe.wait_ge(S.s, n)
+    P(T.b7[:, 8:10], T.e0[:], f("dd", 0, 2), True, False)
+    P(T.b7[:, 8:10], T.e1[:], f("nd", 0, 2), False, False)
+    n_dd = P(T.b7[:, 9:10], T.fm[:], f("nd", 0, 1), False, True)
+
+    for j in range(4):
+        sca.wait_ge(S["xl%d" % j], 16)
     sca.wait_ge(S.v, n_lown)
-    nmx = noff * (3 if direct else 4)
-    for which, src, lst, buf, rk in (("o", T.xs, T.lown, T.so, rank), ("m", T.mx, T.lmir, T.sm, mrank)):
-        if which == "m":
-            sca.wait_ge(S.v, n_lmir)
-            vv()
-            for q in (v, sca):
-                q.wait_ge(S.mxs, nmx)
-        for t in range(8):
-            d = chip.index(order[t])
-            out = T.land[:, SLOT * rk:SLOT * rk + SLOT] if t == 7 else buf[:, SLOT * t:SLOT * t + SLOT]
-            win = src[:, 0:W].indirect(lst[:, 32 * d:32 * d + 17])
-            if t % 2:
-                V(v.tensor_copy(out, win))
-            else:
-                inc("s", sca.activation(out, win, ActivationFunctionType.Copy))
-            done[which, t] = (cnt["v"], cnt["s"])
+    v.wait_ge(S.mxs, noff * (3 if direct else 4))
+    vv()
+    done = []
+    for t in range(8):
+        d, dst, c = chip.index(order[t]), (T.so if t < 7 else T.land), PAIR * (t if t < 7 else ix)
+        C(dst[:, c:c + SLOT], T.xs[:, 0:W].indirect(T.lown[:, 32 * d:32 * d + 17]), AF.Copy)
+        V(v.tensor_copy(dst[:, c + SLOT:c + PAIR], T.mx[:, 0:W].indirect(T.lmir[:, 32 * d:32 * d + 17])))
+        done.append((cnt["v"], cnt["s"]))
 
-    v.wait_ge(S.p, n_srd)
-    V(v.tensor_copy(i("sd"), T.b7[:, 0:1]))
-    V(v.tensor_tensor(f("d1", 0, 2), f("red", 2, 4), T.b5[:, 0:2], A.subtract))
-    V(v.tensor_scalar(f("pq", 0, 2), T.b5[:, 0:2], float(-W * rank), None, A.add))
-    vv()
-    V(v.tensor_scalar(i("sdj"), i("sd"), 0xFFF0, None, A.bitwise_and))
-    V(v.tensor_copy(i("pi", 0, 2), f("pq", 0, 2)))
-    vv()
-    V(v.tensor_copy(f("sdf"), i("sdj")))
-    V(v.tensor_scalar(i("ai", 0, 2), i("pi", 0, 2), 4, None, A.arith_shift_right))
-    V(v.tensor_scalar(i("bi", 0, 2), i("pi", 0, 2), 15, None, A.bitwise_and))
-    vv()
-    n = V(v.tensor_scalar(f("d2", 0, 2), f("d1", 0, 2), f("sdf"), f("rcon"), A.subtract, A.add))
-    V(v.tensor_copy(f("af", 0, 2), i("ai", 0, 2)))
-    V(v.tensor_copy(f("bf", 0, 2), i("bi", 0, 2)))
-    pe.wait_ge(S.v, n)
-    P(T.b7[:, 8:10], T.em[:], f("d2", 0, 2), True, False)
-    n = P(T.b7[:, 9:10], T.fm[:], f("d2", 0, 1), False, True)
-    vv()
+    sca.wait_ge(S.p, n_dd)
+    C(f("h0", 0, 2), T.b7[:, 8:10], bias=BIG, scale=1.0 / 1024)
+    C(f("dc", 0, 2), T.b7[:, 8:10])
+    ss()
+    C(f("h1", 0, 2), f("h0", 0, 2), bias=-BIG)
+    ss()
+    C(f("hh", 0, 2), f("h1", 0, 2), scale=1024.0)
     for h in range(2):
-        V(v.tensor_scalar(T.rl[:, half(h)], T.colq[:], f("af", h, h + 1), None, A.is_gt))
-        V(v.tensor_scalar(T.rl[:, half(2 + h)], T.colq[:], f("af", h, h + 1), None, A.is_equal))
-    v.wait_ge(S.p, n)
-    V(v.tensor_copy(f("dd", 0, 2), T.b7[:, 8:10]))
-    vv()
+        n_lw = C(f("lw", h, h + 1), f("h1", h, h + 1), bias=f("dc", h, h + 1), scale=-1024.0)
+    v.wait_ge(S.s, n_lw)
     for h in range(2):
-        V(v.tensor_scalar(T.ll[:, half(h)], T.colq[:], 0.0, f("dd", h, h + 1), A.is_ge, A.mult))
-        n = V(v.tensor_scalar(T.ll[:, half(2 + h)], T.colm[:], f("bf", h, h + 1), f("dd", h, h + 1), A.is_ge, A.mult))
-    pe.wait_ge(S.v, n)
-    for h in range(4):
-        n = P(T.b0[:, 0:128], T.ll[:, half(h)], T.rl[:, half(h)], h == 0, h == 3)
+        V(v.tensor_scalar(T.rl[:, half(h)], T.colq16[:], f("an", h, h + 1), None, A.is_gt))
+        V(v.tensor_scalar(T.rl[:, half(2 + h)], T.colq16[:], f("an", h, h + 1), None, A.is_equal))
+    pe.wait_ge(S.v, cnt["v"])
+    P(T.b0[:, 0:128], T.ident[:], T.posc[:], True, False)
+    for k, part in enumerate(("hh", "lw")):
+        for h in range(2):
+            a, b = 4 * k + 2 * h, 4 * k + 2 * h + 1
+            V(v.tensor_scalar(T.ll[:, half(a)], T.ones[:], f(part, h, h + 1), None, A.mult))
+            n = V(v.tensor_scalar(T.ll[:, half(b)], T.mrow[:], f("bz", h, h + 1), f(part, h, h + 1), A.is_ge, A.mult))
+            pe.wait_ge(S.v, n)
+            P(T.b0[:, 0:128], T.ll[:, half(a)], T.rl[:, half(h)], False, False)
+            n = P(T.b0[:, 0:128], T.ll[:, half(b)], T.rl[:, half(2 + h)], False, k + h == 2)
     v.wait_ge(S.p, n)
-    V(v.tensor_tensor(T.fi[:], T.b0[:, 0:128], T.posc[:], A.add))
-    vv()
-    n_fu = V(v.tensor_copy(T.fu[:], T.fi[:]))
+    n_fu = V(v.tensor_copy(T.fu[:], T.b0[:, 0:128]))
 
     vv()
-    v.wait_ge(S.landed, 7 * (2 + 4))
+    v.wait_ge(S.s, n_lw)
+    v.wait_ge(S.landed, nland)
     sca.wait_ge(S.v, n_fu)
-    sca.wait_ge(S.landed, 7 * (2 + 4))
+    ss()
+    sca.wait_ge(S.landed, nland)
     ready = []
     for c in range(4):
-        win = T.land[:, 0:16 * SLOT].indirect(T.fu[:, 32 * c:32 * c + 32])
+        win = T.land[:, 0:8 * PAIR].indirect(T.fu[:, 32 * c:32 * c + 32])
         out = T.ys[:, 512 * c:512 * c + 512]
         if c % 2:
-            ready.append(("s", inc("s", sca.activation(out, win, ActivationFunctionType.Copy))))
+            ready.append(("s", C(out, win, AF.Copy)))
         else:
             ready.append(("v", V(v.tensor_copy(out, win))))
     for c, (q, n) in enumerate(ready):
@@ -374,27 +413,28 @@ def rank_program(g, core, T, topo):
         fused([(grp, S.ht, mine, mine, on)])
     g.wait_ge(S.xl1, 16)
     xsend(1, 512, 1024)
+    g.wait_ge(S.xl2, 16)
     if direct:
         g.wait_ge(S.ht, 7 * len(bits(on)))
         blk = T.lt[:, 4 * r0:4 * r0 + 32]
         fused([(tdest(core, far), S.xt, blk, blk, off)])
-    g.wait_ge(S.v, n_slu)
-    send(me if direct else relay[core], S.sls if direct else S.rls, T.slm[:], T.slu[:], off)
-    g.wait_ge(S.xl2, 16)
-    g.wait_ge(S.xl3, 16)
-    if direct:
+        g.wait_ge(S.xl3, 16)
         xsend(2, 1024, 2048)
     else:
         xsend(2, 1024, 1536)
+    g.wait_ge(S.s, n_sl)
+    send(me if direct else relay[core], S.sls if direct else S.rls, T.slx[:, 0:128], T.sl[:, 0:128], off)
+    if not direct:
+        g.wait_ge(S.xl3, 16)
         xsend(3, 1536, 2048)
-    for which, buf, rk, eng, w in (("o", T.so, rank, on, 2), ("m", T.sm, mrank, onall, 4)):
-        ms = deal(eng, 4, w)
-        out = T.land[:, SLOT * rk:SLOT * rk + SLOT]
-        for ts in ((0, 1, 2, 3), (4, 5, 6)):
-            nv, ns = done[which, ts[-1]]
-            g.wait_ge(S.v, nv)
-            g.wait_ge(S.s, ns)
-            fused([([order[t]], S.landed, out, buf[:, SLOT * t:SLOT * t + SLOT], ms[j]) for j, t in enumerate(ts)])
+    t = 0
+    out = T.land[:, PAIR * ix:PAIR * ix + PAIR]
+    for c in calls:
+        nv, ns = done[t + len(c) - 1]
+        g.wait_ge(S.v, nv)
+        g.wait_ge(S.s, ns)
+        fused([([d], S.landed, out, T.so[:, PAIR * (t + j):PAIR * (t + j) + PAIR], m) for j, (d, m) in enumerate(c)])
+        t += len(c)
     g.wait_ge(S.sent, nsent[0])
     g.sync.wait_ge(S.st, 64)
     for q in ("gi", "v", "s", "p"):

@@ -6,7 +6,8 @@ W = 2048
 SLOT = 272
 PAIR = 2 * SLOT
 BIG = 12582912.0
-PIECES = [(0, 512), (512, 1024), (1024, 1536), (1536, 2048)]
+PIECES = [(0, 256), (256, 960), (960, 1664), (1664, 2048)]
+EARLY = 1
 F, H, I, U, B = "float32", "float16", "int32", "uint16", "bfloat16"
 SCRATCH = {
     "xs": ("sbuf", [128, W], B), "mx": ("sbuf", [128, W], B), "ys": ("sbuf", [128, W], B),
@@ -16,13 +17,13 @@ SCRATCH = {
     "colm": ("sbuf", [128, 128], F), "colk": ("sbuf", [128, 128], F), "colq": ("sbuf", [128, 128], F), "dif": ("sbuf", [128, 128], F),
     "oc": ("sbuf", [128, 32], H), "cm": ("sbuf", [128, 16], H),
     "mrow": ("sbuf", [128, 128], H), "colq16": ("sbuf", [128, 128], H),
-    "ones": ("sbuf", [128, 128], H), "mr": ("sbuf", [128, 128], H), "samem": ("sbuf", [128, 128], H), "samem16": ("sbuf", [128, 128], H),
+    "ones": ("sbuf", [128, 128], H), "samem": ("sbuf", [128, 128], H), "samem16": ("sbuf", [128, 128], H),
     "samek": ("sbuf", [128, 128], H), "ltk": ("sbuf", [128, 128], H), "nle": ("sbuf", [128, 128], H), "bm": ("sbuf", [128, 128], H),
-    "samekr": ("sbuf", [128, 128], H), "ltkr": ("sbuf", [128, 128], H), "um": ("sbuf", [128, 128], H), "ident": ("sbuf", [128, 128], H),
+    "um": ("sbuf", [128, 128], H), "ident": ("sbuf", [128, 128], H),
     "selo": ("sbuf", [128, 128], H), "selm": ("sbuf", [128, 128], H),
     "ee": ("sbuf", [128, 256], F), "e0": ("sbuf", [128, 128], F), "e1": ("sbuf", [128, 128], F), "fm": ("sbuf", [128, 128], F),
     "posc": ("sbuf", [128, 128], H),
-    "oh": ("sbuf", [128, 256], H), "sc": ("sbuf", [128, 256], H), "wb": ("sbuf", [128, 256], H), "ow": ("sbuf", [128, 256], H),
+    "oh": ("sbuf", [128, 256], H), "sc": ("sbuf", [128, 256], H), "bs": ("sbuf", [128, 32], H), "ow": ("sbuf", [128, 256], H),
     "lh": ("sbuf", [128, 2048], H), "rh": ("sbuf", [128, 2048], H),
     "sl": ("sbuf", [128, 160], F), "slx": ("sbuf", [128, 160], F),
     "lt": ("sbuf", [128, 64], F), "cc": ("sbuf", [128, 32], H), "cl": ("sbuf", [128, 32], H), "ou": ("sbuf", [128, 32], U),
@@ -33,8 +34,8 @@ for _b in range(8):
     SCRATCH["b%d" % _b] = ("psum", [128, 512], F)
 SEMAPHORES = ["kl", "xl0", "xl1", "xl2", "xl3", "gi", "v", "s", "p", "sent", "ht", "xt", "mxs", "sls", "landed", "st",
               "rl0", "rl1", "rl2", "rl3", "rls"]
-FS = {n: 4 * j for j, n in enumerate(["pm", "pk", "pk8", "sc1", "sc2", "rca", "rcb", "rcon", "red", "z", "d1", "ac", "an", "bz", "s1", "s2",
-                                      "e", "dd", "nd", "dc", "h0", "h1", "hh", "lw"])}
+FS = {n: 4 * j for j, n in enumerate(["pm", "pk", "pk8", "sc1", "sc2", "mk", "rca", "rcb", "rcon", "red", "z", "d1", "ac", "an", "bz",
+                                      "s1", "s2", "e", "dd", "nd", "dc", "h0", "h1", "hh", "lw"])}
 FS.update({"jc": 128, "dcon": 144, "lof": 160, "hif": 176, "tc": 192, "ocf": 224})
 IS = {"ip": 0, "pm": 4, "pk": 8}
 
@@ -69,16 +70,23 @@ def layout(T, topo):
     return mirror, relay
 
 
-def exchange(T, topo, c):
+def exchange(T, topo, c, off):
     here = [a for a in T.cores if same_chip(topo, a, c)]
     own = [a for a in here if topo.die(a) == topo.die(c)]
     oth = [a for a in here if topo.die(a) != topo.die(c)]
     k, n = own.index(c), len(own)
     own = [own[(k + 1 + t) % n] for t in range(n - 1)]
     oth = [oth[(k + t) % n] for t in range(n)]
-    e = bits(topo.mask(c, oth[0]))
-    calls = [[(oth[t], unbits(e[0::2])), (own[t], unbits(e[1::2]))] for t in range(n - 1)]
-    return calls + [[(oth[n - 1], unbits(e))]]
+    full = topo.mask(c, oth[0])
+
+    def call(part, t, m):
+        e = bits(m)
+        if t == n - 1:
+            return (part, [(2 * t, oth[t], unbits(e))])
+        return (part, [(2 * t, oth[t], unbits(e[0::2])), (2 * t + 1, own[t], unbits(e[1::2]))])
+
+    return ([call(0, t, full & ~off) for t in range(EARLY)] + [call(1, t, full) for t in range(EARLY)]
+            + [call(2, t, full) for t in range(EARLY, n)])
 
 
 def rank_program(g, core, T, topo):
@@ -125,22 +133,26 @@ def rank_program(g, core, T, topo):
     r0 = T.rank_of(chip[0])
     mrank = T.rank_of(me)
     direct = core not in relay
+    first = me if direct else relay[core]
     ports = [c for c in chip if c not in relay]
-    off = topo.mask(core, me if direct else relay[core])
+    off = topo.mask(core, first)
     on = topo.mask(core, chip[ix - 1]) & ~off
     noff = len(bits(off))
     peers = [chip[(ix + 1 + t) % 8] for t in range(7)]
-    calls = exchange(T, topo, core)
-    order = [d for c in calls for d, m in c] + [core]
-    nland = sum(len(bits(m)) for p in peers for c in exchange(T, topo, p) for d, m in c if d == core)
+    calls = exchange(T, topo, core, off)
+    order = {t: d for part, c in calls for t, d, m in c}
+    order[7] = core
+    nht = 7 * len(bits(on))
+    nmx = noff * len(PIECES)
+    nland = sum(len(bits(m)) for p in peers for part, c in exchange(T, topo, p, off) for t, d, m in c if d == core)
     place = [PAIR * chip.index(c) if c in chip else PAIR * chip.index(mirror[c]) + SLOT for c in T.cores]
     step = place[8] - place[0] - 8 * PAIR
     assert place == [place[0] + PAIR * r + (step if r >= 8 else 0) for r in range(16)]
 
     def tdest(c, there):
-        pc = [a for a in ports if topo.die(a) == topo.die(c)]
+        owners = [a for a in ports if topo.die(a) == topo.die(c)]
         fd = [a for a in there if topo.die(a) == topo.die(c)]
-        return [d for j, d in enumerate(fd) if pc[j % len(pc)] == c]
+        return [d for j, d in enumerate(fd) if owners[j % len(owners)] == c]
 
     g.sync.dma_start(T.ki[0:16, :], T.key[:]).then_inc(S.kl, 16)
     for j, q in ((0, g.scalar), (1, g.sync), (2, g.scalar), (3, g.sync)):
@@ -177,13 +189,18 @@ def rank_program(g, core, T, topo):
     def half(h):
         return slice(128 * h, 128 * h + 128)
 
+    def xsend(j):
+        a, b = PIECES[j]
+        g.wait_ge(S["xl%d" % j], 16)
+        send(first, S.mxs if direct else S["rl%d" % j], T.mx[:, a:b], T.xs[:, a:b], off)
+
     iota(i("ip"), [[0, 1]], 0, 1)
-    iota(T.colm[:], [[0, 8], [1, 16]], 0, 0)
-    n_m = iota(T.colk[:], [[1, 8], [0, 16]], 0, 0)
+    n_m = iota(T.colm[:], [[0, 8], [1, 16]], 0, 0)
+    n_k = iota(T.colk[:], [[1, 8], [0, 16]], 0, 0)
     n_d = iota(T.dif[:], [[1, 128]], 0, -1)
+    xsend(0)
     iota(T.colq[:], [[1, 128]], 0, 0)
     iota(f("jc", 0, 16), [[1, 16]], 0, 16)
-    iota(f("dcon", 0, 16), [[W, 8], [0, 2]], W * r0, 0)
     n_all = iota(f("ocf", 0, 32), [[0, 16], [16, 2]], 0, 0)
 
     sca.wait_ge(S.gi, n_d)
@@ -197,57 +214,57 @@ def rank_program(g, core, T, topo):
     v.wait_ge(S.gi, n_m)
     V(v.tensor_scalar(i("pm"), i("ip"), 15, None, A.bitwise_and))
     V(v.tensor_scalar(i("pk"), i("ip"), 4, None, A.arith_shift_right))
-    V(v.tensor_scalar(T.mr[:], T.colm[:], float(rank), None, A.is_equal))
     V(v.tensor_scalar(T.ones[:], T.colm[:], 0.0, None, A.is_ge))
     vv()
     V(v.tensor_copy(f("pm"), i("pm")))
     V(v.tensor_copy(f("pk"), i("pk")))
     vv()
     V(v.tensor_scalar(T.samem[:], T.colm[:], f("pm"), None, A.is_equal))
+    V(v.tensor_scalar(f("pk8"), f("pk"), 8.0, None, A.add))
+    V(v.tensor_scalar(f("mk"), f("pm"), float(rank), None, A.is_equal))
+    v.wait_ge(S.gi, n_k)
     V(v.tensor_scalar(T.samek[:], T.colk[:], f("pk"), None, A.is_equal))
     V(v.tensor_scalar(T.ltk[:], T.colk[:], f("pk"), None, A.is_gt))
-    V(v.tensor_scalar(f("pk8"), f("pk"), 8.0, None, A.add))
-    v.wait_ge(S.gi, n_d)
-    V(v.tensor_scalar(T.nle[:], T.dif[:], 0.0, -1.0, A.is_le, A.mult))
-    vv()
-    V(v.tensor_tensor(T.samekr[:], T.samek[:], T.mr[:], A.mult))
-    V(v.tensor_tensor(T.ltkr[:], T.ltk[:], T.mr[:], A.mult))
-    V(v.tensor_tensor(T.bm[:], T.samek[:], T.nle[:], A.mult))
-
     v.wait_ge(S.kl, 16)
     n = V(v.tensor_copy(T.k16[0:16, :], T.ki[0:16, :]))
     pe.wait_ge(S.v, n)
     n = P(T.b0[:, 0:128], T.samem[0:16, :], T.k16[0:16, :], True, True)
+    v.wait_ge(S.gi, n_d)
+    V(v.tensor_scalar(T.nle[:], T.dif[:], 0.0, -1.0, A.is_le, A.mult))
     v.wait_ge(S.p, n)
     V(v.tensor_scalar(T.oh[:, 0:128], T.b0[:, 0:128], f("pk"), None, A.is_equal))
     V(v.tensor_scalar(T.oh[:, 128:256], T.b0[:, 0:128], f("pk8"), None, A.is_equal))
     vv()
     V(v.tensor_tensor_scan(T.sc[:, 0:128], T.ones[:], T.oh[:, 0:128], 0.0, A.mult, A.add))
     n = V(v.tensor_tensor_scan(T.sc[:, 128:256], T.ones[:], T.oh[:, 128:256], 0.0, A.mult, A.add))
+    n_bm = V(v.tensor_tensor(T.bm[:], T.samek[:], T.nle[:], A.mult))
     pe.wait_ge(S.v, n)
     tot = T.sc[:, 127:256:128]
-    P(T.b1[:, 0:2], T.samekr[:], tot, True, True)
-    P(T.b1[:, 2:4], T.ltkr[:], tot, True, False)
-    n_h = P(T.b1[:, 3:4], T.mr[:], T.sc[:, 127:128], False, True)
-    P(T.b3[:, 32:34], T.ltk[:], tot, True, False)
-    P(T.b3[:, 33:34], T.ones[:], T.sc[:, 127:128], False, True)
-    for h in range(2):
-        P(T.b2[:, half(h)], T.samek[:], T.sc[:, half(h)], True, False)
-        n_w = P(T.b2[:, half(h)], T.bm[:], T.oh[:, half(h)], False, True)
+    P(T.b1[:, 0:2], T.samek[:], tot, True, True)
+    P(T.b1[:, 2:4], T.ltk[:], tot, True, False)
+    n_h = P(T.b1[:, 3:4], T.ones[:], T.sc[:, 127:128], False, True)
+    pe.wait_ge(S.v, n_bm)
+    n_w = []
+    for h, bk in ((0, T.b2), (1, T.b5)):
+        P(bk[:, 0:128], T.samek[:], T.sc[:, half(h)], True, False)
+        n_w.append(P(bk[:, 0:128], T.bm[:], T.oh[:, half(h)], False, True))
     v.wait_ge(S.p, n_h)
-    n_hist = V(v.tensor_copy(T.lt[:, 4 * rank:4 * rank + 4], T.b1[:, 0:4]))
+    n_hist = V(v.tensor_scalar(T.lt[:, 4 * rank:4 * rank + 4], T.b1[:, 0:4], f("mk"), None, A.mult))
 
-    v.wait_ge(S.p, n_w)
-    for h in range(2):
-        V(v.tensor_scalar(T.wb[:, half(h)], T.b2[:, half(h)], T.b3[:, 32 + h:33 + h], None, A.add))
     V(v.tensor_scalar(T.samem16[:], T.samem[:], 0.0625, None, A.mult))
     V(v.tensor_scalar(T.cm[:], T.colm[:, 0:16], 0.0, -15.0 / 4096, A.mult, A.add))
     vv()
-    n = V(v.tensor_tensor(T.ow[:], T.wb[:], T.oh[:], A.mult))
-    pe.wait_ge(S.v, n)
-    P(T.b3[:, 0:16], T.ones[:], T.cm[:], True, False)
-    P(T.b3[:, 0:16], T.ow[:, 0:128], T.samem16[:, 0:16], False, False)
-    n = P(T.b3[:, 0:16], T.ow[:, 128:256], T.samem16[:, 0:16], False, True)
+    for h in range(2):
+        V(v.tensor_scalar(T.bs[:, 16 * h:16 * h + 16], T.samem16[:, 0:16], T.b1[:, 2 + h:3 + h], None, A.mult))
+    for h, bk in ((0, T.b2), (1, T.b5)):
+        v.wait_ge(S.p, n_w[h])
+        n = V(v.tensor_tensor(T.ow[:, half(h)], bk[:, 0:128], T.oh[:, half(h)], A.mult))
+        pe.wait_ge(S.v, n)
+        if h == 0:
+            P(T.b3[:, 0:16], T.ones[:], T.cm[:], True, False)
+            P(T.b3[:, 0:16], T.oh[:, 0:128], T.bs[:, 0:16], False, False)
+            P(T.b3[:, 0:16], T.oh[:, 128:256], T.bs[:, 16:32], False, False)
+        n = P(T.b3[:, 0:16], T.ow[:, half(h)], T.samem16[:, 0:16], False, h == 1)
     v.wait_ge(S.gi, n_all)
     V(v.tensor_copy(T.colq16[:], T.colq[:]))
     V(v.tensor_scalar(T.mrow[:], T.colm[:], 0.0625, -0.46875, A.mult, A.add))
@@ -267,6 +284,8 @@ def rank_program(g, core, T, topo):
     sca.wait_ge(S.p, n)
     n_sl = C(T.sl[:, 0:128], T.b4[:, 0:128])
 
+    for t in range(8):
+        V(v.memset(f("dcon", 2 * t, 2 * t + 2), float(W * (r0 + chip.index(order[t])))))
     V(v.tensor_scalar(T.um[:], T.dif[:], 0.0, None, A.is_gt))
     V(v.tensor_scalar(T.ident[:], T.dif[:], 0.0, None, A.is_equal))
     V(v.tensor_scalar(f("sc1"), f("pm"), float(rank), 0.0625, A.is_equal, A.mult))
@@ -280,7 +299,7 @@ def rank_program(g, core, T, topo):
     V(v.tensor_tensor(f("rcon"), f("rca"), f("rcb"), A.add))
     V(v.tensor_scalar(T.posc[:], T.colq[:], 16.0, f("pm"), A.mult, A.add))
 
-    v.wait_ge(S.ht, 7 * len(bits(on)))
+    v.wait_ge(S.ht, nht)
     v.wait_ge(S.xt, noff)
     vv()
     for j in range(2):
@@ -305,17 +324,20 @@ def rank_program(g, core, T, topo):
         P(bk[:, 0:16], sel[:], T.cl[:, 0:16], False, False)
         ns.append(P(bk[:, 0:16], sel[:], T.cl[:, 16:32], False, True))
     P(T.b7[:, 0:1], T.ones[:], T.cm[:, 0:1], True, False)
-    P(T.b7[:, 0:1], T.samem16[:], T.cl[:, 2 * ix:2 * ix + 1], False, False)
-    n_srd = P(T.b7[:, 0:1], T.samem16[:], T.cl[:, 16 + 2 * ix:17 + 2 * ix], False, True)
+    P(T.b7[:, 0:1], T.samem16[:], T.cl[:, 14:15], False, False)
+    n_srd = P(T.b7[:, 0:1], T.samem16[:], T.cl[:, 30:31], False, True)
     v.wait_ge(S.p, ns[0])
     n1 = V(v.tensor_scalar(T.ou[:, 0:16], T.b6[:, 0:16], BIG, -BIG, A.add, A.add))
+    v.wait_ge(S.s, n_sl)
+    v.wait_ge(S.v, n1)
+    n_lown = [V(v.tensor_copy(T.lown[:, 0:128], T.sl[:, 0:160].indirect(T.ou[:, 0:8])))]
     v.wait_ge(S.p, ns[1])
     n2 = V(v.tensor_scalar(T.ou[:, 16:32], T.b2[:, 0:16], BIG, -BIG, A.add, A.add))
-    v.wait_ge(S.s, n_sl)
+    n_lown.append(V(v.tensor_copy(T.lown[:, 128:256], T.sl[:, 0:160].indirect(T.ou[:, 8:16]))))
     v.wait_ge(S.v, n2)
-    n_lown = V(v.tensor_copy(T.lown[:], T.sl[:, 0:160].indirect(T.ou[:, 0:16])))
     v.wait_ge(S.sls, noff)
-    n_lmir = V(v.tensor_copy(T.lmir[:], T.slx[:, 0:160].indirect(T.ou[:, 16:32])))
+    V(v.tensor_copy(T.lmir[:, 0:128], T.slx[:, 0:160].indirect(T.ou[:, 16:24])))
+    n_lmir = V(v.tensor_copy(T.lmir[:, 128:256], T.slx[:, 0:160].indirect(T.ou[:, 24:32])))
 
     sca.wait_ge(S.p, n_p)
     C(f("z", 0, 2), T.b1[:, 8:10], bias=-0.46875 - W * rank / 16.0, scale=0.0625)
@@ -326,11 +348,31 @@ def rank_program(g, core, T, topo):
     C(f("ac", 0, 2), f("z", 0, 2), bias=BIG)
     ss()
     C(f("an", 0, 2), f("ac", 0, 2), bias=-BIG)
+    ss()
+    for h in range(2):
+        n_bz = C(f("bz", h, h + 1), f("an", h, h + 1), bias=f("z", h, h + 1), scale=-1.0)
+
+    def slot(t, part):
+        buf, a = (T.so, PAIR * t) if t < 7 else (T.land, PAIR * ix)
+        return buf[:, a:a + PAIR] if part == 2 else buf[:, a + SLOT * part:a + SLOT * part + SLOT]
+
+    def fill(h, t):
+        return (T.mx if h else T.xs)[:, 0:W].indirect((T.lmir if h else T.lown)[:, 32 * t:32 * t + 17])
+
+    for j in range(4):
+        sca.wait_ge(S["xl%d" % j], 16)
+    sca.wait_ge(S.v, n_lown[0])
+    v.wait_ge(S.mxs, nmx)
+    vv()
+    shared = 1 if direct else 2
+    done = {}
+    for t in range(7 - shared):
+        done[t, 1] = ("v", V(v.tensor_copy(slot(t, 1), fill(1, t))))
+    for t in range(4):
+        done[t, 0] = ("s", C(slot(t, 0), fill(0, t), AF.Copy))
     sca.wait_ge(S.p, n_srd)
     C(f("s1"), T.b7[:, 0:1], bias=BIG)
     ss()
-    for h in range(2):
-        C(f("bz", h, h + 1), f("an", h, h + 1), bias=f("z", h, h + 1), scale=-1.0)
     C(f("s2"), f("s1"), bias=-BIG)
     ss()
     C(f("e"), f("s2"), bias=f("rcon"), scale=-16.0)
@@ -342,18 +384,13 @@ def rank_program(g, core, T, topo):
     P(T.b7[:, 8:10], T.e0[:], f("dd", 0, 2), True, False)
     P(T.b7[:, 8:10], T.e1[:], f("nd", 0, 2), False, False)
     n_dd = P(T.b7[:, 9:10], T.fm[:], f("nd", 0, 1), False, True)
-
-    for j in range(4):
-        sca.wait_ge(S["xl%d" % j], 16)
-    sca.wait_ge(S.v, n_lown)
-    v.wait_ge(S.mxs, noff * (3 if direct else 4))
-    vv()
-    done = []
-    for t in range(8):
-        d, dst, c = chip.index(order[t]), (T.so if t < 7 else T.land), PAIR * (t if t < 7 else ix)
-        C(dst[:, c:c + SLOT], T.xs[:, 0:W].indirect(T.lown[:, 32 * d:32 * d + 17]), AF.Copy)
-        V(v.tensor_copy(dst[:, c + SLOT:c + PAIR], T.mx[:, 0:W].indirect(T.lmir[:, 32 * d:32 * d + 17])))
-        done.append((cnt["v"], cnt["s"]))
+    sca.wait_ge(S.v, n_lown[1])
+    for t in range(4, 7):
+        done[t, 0] = ("s", C(slot(t, 0), fill(0, t), AF.Copy))
+    sca.wait_ge(S.v, n_lmir)
+    sca.wait_ge(S.mxs, nmx)
+    for t in range(7 - shared, 7):
+        done[t, 1] = ("s", C(slot(t, 1), fill(1, t), AF.Copy))
 
     sca.wait_ge(S.p, n_dd)
     C(f("h0", 0, 2), T.b7[:, 8:10], bias=BIG, scale=1.0 / 1024)
@@ -364,12 +401,15 @@ def rank_program(g, core, T, topo):
     C(f("hh", 0, 2), f("h1", 0, 2), scale=1024.0)
     for h in range(2):
         n_lw = C(f("lw", h, h + 1), f("h1", h, h + 1), bias=f("dc", h, h + 1), scale=-1024.0)
-    v.wait_ge(S.s, n_lw)
+    for h in range(2):
+        n_self = C(slot(7, h), fill(h, 7), AF.Copy)
+    v.wait_ge(S.s, n_bz)
     for h in range(2):
         V(v.tensor_scalar(T.rl[:, half(h)], T.colq16[:], f("an", h, h + 1), None, A.is_gt))
         V(v.tensor_scalar(T.rl[:, half(2 + h)], T.colq16[:], f("an", h, h + 1), None, A.is_equal))
     pe.wait_ge(S.v, cnt["v"])
     P(T.b0[:, 0:128], T.ident[:], T.posc[:], True, False)
+    v.wait_ge(S.s, n_lw)
     for k, part in enumerate(("hh", "lw")):
         for h in range(2):
             a, b = 4 * k + 2 * h, 4 * k + 2 * h + 1
@@ -382,7 +422,7 @@ def rank_program(g, core, T, topo):
     n_fu = V(v.tensor_copy(T.fu[:], T.b0[:, 0:128]))
 
     vv()
-    v.wait_ge(S.s, n_lw)
+    v.wait_ge(S.s, n_self)
     v.wait_ge(S.landed, nland)
     sca.wait_ge(S.v, n_fu)
     ss()
@@ -399,43 +439,26 @@ def rank_program(g, core, T, topo):
         g.sync.wait_ge(S[q], n)
         g.sync.dma_start(T.y[:, 512 * c:512 * c + 512], T.ys[:, 512 * c:512 * c + 512]).then_inc(S.st, 16)
 
-    def xsend(j, a, b):
-        if direct:
-            send(me, S.mxs, T.mx[:, a:b], T.xs[:, a:b], off)
-        else:
-            send(relay[core], S["rl%d" % j], T.mx[:, a:b], T.xs[:, a:b], off)
-
-    g.wait_ge(S.xl0, 16)
-    xsend(0, 0, 512)
     g.wait_ge(S.v, n_hist)
     mine = T.lt[:, 4 * rank:4 * rank + 4]
-    for grp in ([c for c in peers if c in ports], [c for c in peers if c not in ports]):
-        fused([(grp, S.ht, mine, mine, on)])
-    g.wait_ge(S.xl1, 16)
-    xsend(1, 512, 1024)
-    g.wait_ge(S.xl2, 16)
+    fused([([c for c in peers if c in ports], S.ht, mine, mine, on)])
+    fused([([c for c in peers if c not in ports], S.ht, mine, mine, on)])
+    xsend(1)
     if direct:
-        g.wait_ge(S.ht, 7 * len(bits(on)))
+        g.wait_ge(S.ht, nht)
         blk = T.lt[:, 4 * r0:4 * r0 + 32]
         fused([(tdest(core, far), S.xt, blk, blk, off)])
-        g.wait_ge(S.xl3, 16)
-        xsend(2, 1024, 2048)
-    else:
-        xsend(2, 1024, 1536)
+    xsend(2)
     g.wait_ge(S.s, n_sl)
-    send(me if direct else relay[core], S.sls if direct else S.rls, T.slx[:, 0:128], T.sl[:, 0:128], off)
-    if not direct:
-        g.wait_ge(S.xl3, 16)
-        xsend(3, 1536, 2048)
-    t = 0
-    out = T.land[:, PAIR * ix:PAIR * ix + PAIR]
-    for c in calls:
-        nv, ns = done[t + len(c) - 1]
-        g.wait_ge(S.v, nv)
-        g.wait_ge(S.s, ns)
-        fused([([d], S.landed, out, T.so[:, PAIR * (t + j):PAIR * (t + j) + PAIR], m) for j, (d, m) in enumerate(c)])
-        t += len(c)
+    send(first, S.sls if direct else S.rls, T.slx[:, 0:128], T.sl[:, 0:128], off)
+    xsend(3)
+    for part, c in calls:
+        for t, d, m in c:
+            for h in (0, 1):
+                if part in (h, 2):
+                    g.wait_ge(S[done[t, h][0]], done[t, h][1])
+        fused([([d], S.landed, slot(7, part), slot(t, part), m) for t, d, m in c])
     g.wait_ge(S.sent, nsent[0])
-    g.sync.wait_ge(S.st, 64)
+    g.sync.wait_ge(S.st, 16 * len(ready))
     for q in ("gi", "v", "s", "p"):
         g.sync.wait_ge(S[q], cnt[q])

import numpy as np
from concourse.bass import DstId, RemoteDMATransfer
from concourse.mybir import dt, AluOpType, AxisListType, ActivationFunctionType

W = 2048
SLOT = 272
PAIR = 2 * SLOT
BIG = 12582912.0
PIECES = [(0, 256), (256, 960), (960, 1664), (1664, 2048)]
EARLY = 1
F, H, I, U, B = "float32", "float16", "int32", "uint16", "bfloat16"
SCRATCH = {
    "xs": ("sbuf", [128, W], B), "mx": ("sbuf", [128, W], B), "ys": ("sbuf", [128, W], B),
    "so": ("sbuf", [128, 7 * PAIR], B), "land": ("sbuf", [128, 8 * PAIR], B),
    "ki": ("sbuf", [128, 128], I), "k16": ("sbuf", [128, 128], H),
    "fs": ("sbuf", [128, 384], F), "ints": ("sbuf", [128, 16], I),
    "colm": ("sbuf", [128, 128], F), "colk": ("sbuf", [128, 128], F), "colq": ("sbuf", [128, 128], F), "dif": ("sbuf", [128, 128], F),
    "oc": ("sbuf", [128, 32], H), "cm": ("sbuf", [128, 16], H),
    "mrow": ("sbuf", [128, 128], H), "colq16": ("sbuf", [128, 128], H),
    "ones": ("sbuf", [128, 128], H), "samem": ("sbuf", [128, 128], H), "samem16": ("sbuf", [128, 128], H),
    "samek": ("sbuf", [128, 128], H), "ltk": ("sbuf", [128, 128], H), "nle": ("sbuf", [128, 128], H), "bm": ("sbuf", [128, 128], H),
    "um": ("sbuf", [128, 128], H), "ident": ("sbuf", [128, 128], H),
    "selo": ("sbuf", [128, 128], H), "selm": ("sbuf", [128, 128], H),
    "ee": ("sbuf", [128, 256], F), "e0": ("sbuf", [128, 128], F), "e1": ("sbuf", [128, 128], F), "fm": ("sbuf", [128, 128], F),
    "posc": ("sbuf", [128, 128], H),
    "oh": ("sbuf", [128, 256], H), "sc": ("sbuf", [128, 256], H), "bs": ("sbuf", [128, 32], H), "ow": ("sbuf", [128, 256], H),
    "lh": ("sbuf", [128, 2048], H), "rh": ("sbuf", [128, 2048], H),
    "sl": ("sbuf", [128, 160], F), "slx": ("sbuf", [128, 160], F),
    "lt": ("sbuf", [128, 64], F), "cc": ("sbuf", [128, 32], H), "cl": ("sbuf", [128, 32], H), "ou": ("sbuf", [128, 32], U),
    "lown": ("sbuf", [128, 256], U), "lmir": ("sbuf", [128, 256], U),
    "rl": ("sbuf", [128, 512], H), "ll": ("sbuf", [128, 1024], H), "fu": ("sbuf", [128, 128], U),
}
for _b in range(8):
    SCRATCH["b%d" % _b] = ("psum", [128, 512], F)
SEMAPHORES = ["kl", "xl0", "xl1", "xl2", "xl3", "gi", "v", "s", "p", "sent", "ht", "xt", "mxs", "sls", "landed", "st",
              "rl0", "rl1", "rl2", "rl3", "rls"]
FS = {n: 4 * j for j, n in enumerate(["pm", "pk", "pk8", "sc1", "sc2", "mk", "rca", "rcb", "rcon", "red", "z", "d1", "ac", "an", "bz",
                                      "s1", "s2", "e", "dd", "nd", "dc", "h0", "h1", "hh", "lw"])}
FS.update({"jc": 128, "dcon": 144, "lof": 160, "hif": 176, "tc": 192, "ocf": 224})
IS = {"ip": 0, "pm": 4, "pk": 8}


def bits(m):
    return [b for b in range(m.bit_length()) if m >> b & 1]


def unbits(e):
    return sum(1 << b for b in e)


def same_chip(topo, a, b):
    return (topo.host(a), topo.chip(a)) == (topo.host(b), topo.chip(b))


def layout(T, topo):
    mirror, relay, used = {}, {}, []
    for c in T.cores:
        mine = [a for a in T.cores if same_chip(topo, a, c) and topo.die(a) == topo.die(c)]
        far = [a for a in T.cores if not same_chip(topo, a, c) and topo.die(a) == topo.die(c)]
        mirror[c] = far[mine.index(c)]
    for c in T.cores:
        m = mirror[c]
        if topo.may_write(c, m):
            continue
        for z in range(256):
            if z not in used and topo.mates(z, m) and topo.die(z) == topo.die(c) and topo.may_write(c, z) and topo.may_write(z, m):
                relay[c] = z
                used.append(z)
                break
    return mirror, relay


def exchange(T, topo, c, off):
    here = [a for a in T.cores if same_chip(topo, a, c)]
    own = [a for a in here if topo.die(a) == topo.die(c)]
    oth = [a for a in here if topo.die(a) != topo.die(c)]
    k, n = own.index(c), len(own)
    own = [own[(k + 1 + t) % n] for t in range(n - 1)]
    oth = [oth[(k + t) % n] for t in range(n)]
    full = topo.mask(c, oth[0])

    def call(part, t, m):
        e = bits(m)
        if t == n - 1:
            return (part, [(2 * t, oth[t], unbits(e))])
        return (part, [(2 * t, oth[t], unbits(e[0::2])), (2 * t + 1, own[t], unbits(e[1::2]))])

    return ([call(0, t, full & ~off) for t in range(EARLY)] + [call(1, t, full) for t in range(EARLY)]
            + [call(2, t, full) for t in range(EARLY, n)])


def rank_program(g, core, T, topo):
    A, S, AF = AluOpType, T.sem, ActivationFunctionType
    mirror, relay = layout(T, topo)
    rank = T.rank_of(core)
    nsent = [0]

    def send(dst, sem, out, src, mask):
        rid, pid = topo.addr(dst, core)
        g.remote_dma(out_ap=out, in_ap=src, remote_sem=sem, local_sem=S.sent, pid=pid, routing_id=rid, dma_engine_mask=mask)
        nsent[0] += len(bits(mask))

    def fused(trs):
        g.remote_dma_fused([RemoteDMATransfer(
            dst_ids=[DstId(rid=topo.addr(d, core)[0], pnc=topo.addr(d, core)[1]) for d in ds],
            dma_engine_mask=mask, remote_sem=sem, srcs=[src], dsts=[out] * len(ds)) for ds, sem, out, src, mask in trs], local_sem=S.sent)
        nsent[0] += sum(len(bits(t[4])) for t in trs)

    if rank is None:
        for c in relay:
            if relay[c] != core:
                continue
            n, k, m = len(bits(topo.mask(c, core))), topo.mask(core, mirror[c]), mirror[c]
            for j, (a, b) in enumerate(PIECES):
                if j == 3:
                    g.wait_ge(S.rls, n)
                    send(m, S.sls, T.slx[:, 0:128], T.slx[:, 0:128], k)
                g.wait_ge(S["rl%d" % j], n)
                send(m, S.mxs, T.mx[:, a:b], T.mx[:, a:b], k)
            g.wait_ge(S.sent, nsent[0])
        return

    def f(name, a=0, b=1):
        return T.fs[:, FS[name] + a:FS[name] + b]

    def i(name):
        return T.ints[:, IS[name]:IS[name] + 1]

    me = mirror[core]
    chip = [c for c in T.cores if same_chip(topo, c, core)]
    far = [c for c in T.cores if not same_chip(topo, c, core)]
    ix = chip.index(core)
    r0 = T.rank_of(chip[0])
    mrank = T.rank_of(me)
    direct = core not in relay
    first = me if direct else relay[core]
    ports = [c for c in chip if c not in relay]
    off = topo.mask(core, first)
    on = topo.mask(core, chip[ix - 1]) & ~off
    noff = len(bits(off))
    peers = [chip[(ix + 1 + t) % 8] for t in range(7)]
    calls = exchange(T, topo, core, off)
    order = {t: d for part, c in calls for t, d, m in c}
    order[7] = core
    nht = 7 * len(bits(on))
    nmx = noff * len(PIECES)
    nland = sum(len(bits(m)) for p in peers for part, c in exchange(T, topo, p, off) for t, d, m in c if d == core)
    place = [PAIR * chip.index(c) if c in chip else PAIR * chip.index(mirror[c]) + SLOT for c in T.cores]
    step = place[8] - place[0] - 8 * PAIR
    assert place == [place[0] + PAIR * r + (step if r >= 8 else 0) for r in range(16)]

    def tdest(c, there):
        owners = [a for a in ports if topo.die(a) == topo.die(c)]
        fd = [a for a in there if topo.die(a) == topo.die(c)]
        return [d for j, d in enumerate(fd) if owners[j % len(owners)] == c]

    g.sync.dma_start(T.ki[0:16, :], T.key[:]).then_inc(S.kl, 16)
    for j, q in ((0, g.scalar), (1, g.sync), (2, g.scalar), (3, g.sync)):
        a, b = PIECES[j]
        q.dma_start(T.xs[:, a:b], T.x[:, a:b]).then_inc(S["xl%d" % j], 16)

    cnt = {"gi": 0, "v": 0, "s": 0, "p": 0}

    def inc(q, ins):
        ins.then_inc(S[q], 1)
        cnt[q] += 1
        return cnt[q]

    v, pe, sca = g.vector, g.tensor, g.scalar

    def V(ins):
        return inc("v", ins)

    def P(*a):
        return inc("p", pe.matmul(*a))

    def C(out, in_, func=AF.Identity, bias=0.0, scale=1.0):
        return inc("s", sca.activation(out, in_, func, bias=bias, scale=scale))

    def vv():
        v.wait_ge(S.v, cnt["v"])

    def ss():
        sca.wait_ge(S.s, cnt["s"])

    def iota(out, pattern, base, cm):
        return inc("gi", g.iota(out, pattern, base, cm, allow_small_or_imprecise_dtypes=True))

    def half(h):
        return slice(128 * h, 128 * h + 128)

    def xsend(j):
        a, b = PIECES[j]
        g.wait_ge(S["xl%d" % j], 16)
        send(first, S.mxs if direct else S["rl%d" % j], T.mx[:, a:b], T.xs[:, a:b], off)

    iota(i("ip"), [[0, 1]], 0, 1)
    n_m = iota(T.colm[:], [[0, 8], [1, 16]], 0, 0)
    n_k = iota(T.colk[:], [[1, 8], [0, 16]], 0, 0)
    n_d = iota(T.dif[:], [[1, 128]], 0, -1)
    xsend(0)
    iota(T.colq[:], [[1, 128]], 0, 0)
    iota(f("jc", 0, 16), [[1, 16]], 0, 16)
    n_all = iota(f("ocf", 0, 32), [[0, 16], [16, 2]], 0, 0)

    sca.wait_ge(S.gi, n_d)
    C(T.ee[:, 0:128], T.dif[:], AF.Abs)
    C(T.ee[:, 128:256], T.dif[:], AF.Abs, bias=-1.0)
    C(T.fm[:], T.dif[:], AF.Relu, bias=-126.0, scale=-1.0)
    ss()
    C(T.e0[:], T.ee[:, 0:128], AF.Relu, bias=1.0, scale=-1.0)
    C(T.e1[:], T.ee[:, 128:256], AF.Relu, bias=1.0, scale=-1.0)

    v.wait_ge(S.gi, n_m)
    V(v.tensor_scalar(i("pm"), i("ip"), 15, None, A.bitwise_and))
    V(v.tensor_scalar(i("pk"), i("ip"), 4, None, A.arith_shift_right))
    V(v.tensor_scalar(T.ones[:], T.colm[:], 0.0, None, A.is_ge))
    vv()
    V(v.tensor_copy(f("pm"), i("pm")))
    V(v.tensor_copy(f("pk"), i("pk")))
    vv()
    V(v.tensor_scalar(T.samem[:], T.colm[:], f("pm"), None, A.is_equal))
    V(v.tensor_scalar(f("pk8"), f("pk"), 8.0, None, A.add))
    V(v.tensor_scalar(f("mk"), f("pm"), float(rank), None, A.is_equal))
    v.wait_ge(S.gi, n_k)
    V(v.tensor_scalar(T.samek[:], T.colk[:], f("pk"), None, A.is_equal))
    V(v.tensor_scalar(T.ltk[:], T.colk[:], f("pk"), None, A.is_gt))
    v.wait_ge(S.kl, 16)
    n = V(v.tensor_copy(T.k16[0:16, :], T.ki[0:16, :]))
    pe.wait_ge(S.v, n)
    n = P(T.b0[:, 0:128], T.samem[0:16, :], T.k16[0:16, :], True, True)
    v.wait_ge(S.gi, n_d)
    V(v.tensor_scalar(T.nle[:], T.dif[:], 0.0, -1.0, A.is_le, A.mult))
    v.wait_ge(S.p, n)
    V(v.tensor_scalar(T.oh[:, 0:128], T.b0[:, 0:128], f("pk"), None, A.is_equal))
    V(v.tensor_scalar(T.oh[:, 128:256], T.b0[:, 0:128], f("pk8"), None, A.is_equal))
    vv()
    V(v.tensor_tensor_scan(T.sc[:, 0:128], T.ones[:], T.oh[:, 0:128], 0.0, A.mult, A.add))
    n = V(v.tensor_tensor_scan(T.sc[:, 128:256], T.ones[:], T.oh[:, 128:256], 0.0, A.mult, A.add))
    n_bm = V(v.tensor_tensor(T.bm[:], T.samek[:], T.nle[:], A.mult))
    pe.wait_ge(S.v, n)
    tot = T.sc[:, 127:256:128]
    P(T.b1[:, 0:2], T.samek[:], tot, True, True)
    P(T.b1[:, 2:4], T.ltk[:], tot, True, False)
    n_h = P(T.b1[:, 3:4], T.ones[:], T.sc[:, 127:128], False, True)
    pe.wait_ge(S.v, n_bm)
    n_w = []
    for h, bk in ((0, T.b2), (1, T.b5)):
        P(bk[:, 0:128], T.samek[:], T.sc[:, half(h)], True, False)
        n_w.append(P(bk[:, 0:128], T.bm[:], T.oh[:, half(h)], False, True))
    v.wait_ge(S.p, n_h)
    n_hist = V(v.tensor_scalar(T.lt[:, 4 * rank:4 * rank + 4], T.b1[:, 0:4], f("mk"), None, A.mult))

    V(v.tensor_scalar(T.samem16[:], T.samem[:], 0.0625, None, A.mult))
    V(v.tensor_scalar(T.cm[:], T.colm[:, 0:16], 0.0, -15.0 / 4096, A.mult, A.add))
    vv()
    for h in range(2):
        V(v.tensor_scalar(T.bs[:, 16 * h:16 * h + 16], T.samem16[:, 0:16], T.b1[:, 2 + h:3 + h], None, A.mult))
    for h, bk in ((0, T.b2), (1, T.b5)):
        v.wait_ge(S.p, n_w[h])
        n = V(v.tensor_tensor(T.ow[:, half(h)], bk[:, 0:128], T.oh[:, half(h)], A.mult))
        pe.wait_ge(S.v, n)
        if h == 0:
            P(T.b3[:, 0:16], T.ones[:], T.cm[:], True, False)
            P(T.b3[:, 0:16], T.oh[:, 0:128], T.bs[:, 0:16], False, False)
            P(T.b3[:, 0:16], T.oh[:, 128:256], T.bs[:, 16:32], False, False)
        n = P(T.b3[:, 0:16], T.ow[:, half(h)], T.samem16[:, 0:16], False, h == 1)
    v.wait_ge(S.gi, n_all)
    V(v.tensor_copy(T.colq16[:], T.colq[:]))
    V(v.tensor_scalar(T.mrow[:], T.colm[:], 0.0625, -0.46875, A.mult, A.add))
    V(v.memset(T.sl[:, 128:160], 0.0))
    V(v.memset(T.slx[:, 128:160], 0.0))
    v.wait_ge(S.p, n)
    V(v.tensor_scalar(f("hif", 0, 16), T.b3[:, 0:16], BIG, -BIG, A.add, A.add))
    vv()
    V(v.tensor_tensor(f("lof", 0, 16), T.b3[:, 0:16], f("hif", 0, 16), A.subtract))
    for m in range(16):
        V(v.tensor_scalar(T.rh[:, half(m)], T.colq16[:], f("hif", m, m + 1), None, A.is_equal))
        if m == 0:
            vv()
        n = V(v.tensor_scalar(T.lh[:, half(m)], T.mrow[:], f("lof", m, m + 1), f("jc", m, m + 1), A.is_equal, A.mult))
        pe.wait_ge(S.v, n)
        n = P(T.b4[:, 0:128], T.lh[:, half(m)], T.rh[:, half(m)], m == 0, m == 15)
    sca.wait_ge(S.p, n)
    n_sl = C(T.sl[:, 0:128], T.b4[:, 0:128])

    for t in range(8):
        V(v.memset(f("dcon", 2 * t, 2 * t + 2), float(W * (r0 + chip.index(order[t])))))
    V(v.tensor_scalar(T.um[:], T.dif[:], 0.0, None, A.is_gt))
    V(v.tensor_scalar(T.ident[:], T.dif[:], 0.0, None, A.is_equal))
    V(v.tensor_scalar(f("sc1"), f("pm"), float(rank), 0.0625, A.is_equal, A.mult))
    V(v.tensor_scalar(f("sc2"), f("pm"), float(mrank), 0.0625, A.is_equal, A.mult))
    V(v.tensor_scalar(T.oc[:], f("ocf", 0, 32), f("pm"), -0.46875, A.add, A.add))
    V(v.tensor_scalar(f("rca"), f("pm"), 8.0, float(step), A.is_ge, A.mult))
    V(v.tensor_scalar(f("rcb"), f("pm"), float(PAIR), float(place[0] + W * rank), A.mult, A.add))
    vv()
    V(v.tensor_scalar(T.selo[:], T.ones[:], f("sc1"), None, A.mult))
    V(v.tensor_scalar(T.selm[:], T.ones[:], f("sc2"), None, A.mult))
    V(v.tensor_tensor(f("rcon"), f("rca"), f("rcb"), A.add))
    V(v.tensor_scalar(T.posc[:], T.colq[:], 16.0, f("pm"), A.mult, A.add))

    v.wait_ge(S.ht, nht)
    v.wait_ge(S.xt, noff)
    vv()
    for j in range(2):
        n = V(v.tensor_tensor_scan(T.cc[:, 16 * j:16 * j + 16], T.ones[:, 0:16], T.lt[:, j:64:4], 0.0, A.mult, A.add))
    for j in range(4):
        n_red = V(v.tensor_reduce(f("red", j, j + 1), T.lt[:, j:64:4], AxisListType.X, A.add))
    pe.wait_ge(S.v, n)
    for bk, c in ((T.b5, 0), (T.b1, 8)):
        P(bk[:, c:c + 2], T.um[:], T.cc[:, 15:32:16], True, False)
        n_p = P(bk[:, c + 1:c + 2], T.ones[:], T.cc[:, 15:16], False, True)
        if c == 0:
            v.wait_ge(S.p, n_p)
    for h in range(2):
        V(v.tensor_scalar(f("tc", 16 * h, 16 * h + 16), f("dcon", 0, 16), T.b5[:, h:h + 1], 0.0, A.subtract, A.max))
    vv()
    for h in range(2):
        n = V(v.tensor_scalar(T.cl[:, 16 * h:16 * h + 16], f("tc", 16 * h, 16 * h + 16), f("red", h, h + 1), None, A.min))
    pe.wait_ge(S.v, n)
    ns = []
    for bk, sel in ((T.b6, T.selo), (T.b2, T.selm)):
        P(bk[:, 0:16], T.ident[:], T.oc[:, 0:16], True, False)
        P(bk[:, 0:16], sel[:], T.cl[:, 0:16], False, False)
        ns.append(P(bk[:, 0:16], sel[:], T.cl[:, 16:32], False, True))
    P(T.b7[:, 0:1], T.ones[:], T.cm[:, 0:1], True, False)
    P(T.b7[:, 0:1], T.samem16[:], T.cl[:, 14:15], False, False)
    n_srd = P(T.b7[:, 0:1], T.samem16[:], T.cl[:, 30:31], False, True)
    v.wait_ge(S.p, ns[0])
    n1 = V(v.tensor_scalar(T.ou[:, 0:16], T.b6[:, 0:16], BIG, -BIG, A.add, A.add))
    v.wait_ge(S.s, n_sl)
    v.wait_ge(S.v, n1)
    n_lown = [V(v.tensor_copy(T.lown[:, 0:128], T.sl[:, 0:160].indirect(T.ou[:, 0:8])))]
    v.wait_ge(S.p, ns[1])
    n2 = V(v.tensor_scalar(T.ou[:, 16:32], T.b2[:, 0:16], BIG, -BIG, A.add, A.add))
    n_lown.append(V(v.tensor_copy(T.lown[:, 128:256], T.sl[:, 0:160].indirect(T.ou[:, 8:16]))))
    v.wait_ge(S.v, n2)
    v.wait_ge(S.sls, noff)
    V(v.tensor_copy(T.lmir[:, 0:128], T.slx[:, 0:160].indirect(T.ou[:, 16:24])))
    n_lmir = V(v.tensor_copy(T.lmir[:, 128:256], T.slx[:, 0:160].indirect(T.ou[:, 24:32])))

    sca.wait_ge(S.p, n_p)
    C(f("z", 0, 2), T.b1[:, 8:10], bias=-0.46875 - W * rank / 16.0, scale=0.0625)
    sca.wait_ge(S.v, n_red)
    for h in range(2):
        C(f("d1", h, h + 1), T.b1[:, 8 + h:9 + h], bias=f("red", 2 + h, 3 + h), scale=-1.0)
    ss()
    C(f("ac", 0, 2), f("z", 0, 2), bias=BIG)
    ss()
    C(f("an", 0, 2), f("ac", 0, 2), bias=-BIG)
    ss()
    for h in range(2):
        n_bz = C(f("bz", h, h + 1), f("an", h, h + 1), bias=f("z", h, h + 1), scale=-1.0)

    def slot(t, part):
        buf, a = (T.so, PAIR * t) if t < 7 else (T.land, PAIR * ix)
        return buf[:, a:a + PAIR] if part == 2 else buf[:, a + SLOT * part:a + SLOT * part + SLOT]

    def fill(h, t):
        return (T.mx if h else T.xs)[:, 0:W].indirect((T.lmir if h else T.lown)[:, 32 * t:32 * t + 17])

    for j in range(4):
        sca.wait_ge(S["xl%d" % j], 16)
    sca.wait_ge(S.v, n_lown[0])
    v.wait_ge(S.mxs, nmx)
    vv()
    shared = 1 if direct else 2
    done = {}
    for t in range(7 - shared):
        done[t, 1] = ("v", V(v.tensor_copy(slot(t, 1), fill(1, t))))
    for t in range(4):
        done[t, 0] = ("s", C(slot(t, 0), fill(0, t), AF.Copy))
    sca.wait_ge(S.p, n_srd)
    C(f("s1"), T.b7[:, 0:1], bias=BIG)
    ss()
    C(f("s2"), f("s1"), bias=-BIG)
    ss()
    C(f("e"), f("s2"), bias=f("rcon"), scale=-16.0)
    ss()
    C(f("dd", 0, 2), f("d1", 0, 2), bias=f("e"))
    ss()
    n = C(f("nd", 0, 2), f("dd", 0, 2), scale=-1.0)
    pe.wait_ge(S.s, n)
    P(T.b7[:, 8:10], T.e0[:], f("dd", 0, 2), True, False)
    P(T.b7[:, 8:10], T.e1[:], f("nd", 0, 2), False, False)
    n_dd = P(T.b7[:, 9:10], T.fm[:], f("nd", 0, 1), False, True)
    sca.wait_ge(S.v, n_lown[1])
    for t in range(4, 7):
        done[t, 0] = ("s", C(slot(t, 0), fill(0, t), AF.Copy))
    sca.wait_ge(S.v, n_lmir)
    sca.wait_ge(S.mxs, nmx)
    for t in range(7 - shared, 7):
        done[t, 1] = ("s", C(slot(t, 1), fill(1, t), AF.Copy))

    sca.wait_ge(S.p, n_dd)
    C(f("h0", 0, 2), T.b7[:, 8:10], bias=BIG, scale=1.0 / 1024)
    C(f("dc", 0, 2), T.b7[:, 8:10])
    ss()
    C(f("h1", 0, 2), f("h0", 0, 2), bias=-BIG)
    ss()
    C(f("hh", 0, 2), f("h1", 0, 2), scale=1024.0)
    for h in range(2):
        n_lw = C(f("lw", h, h + 1), f("h1", h, h + 1), bias=f("dc", h, h + 1), scale=-1024.0)
    for h in range(2):
        n_self = C(slot(7, h), fill(h, 7), AF.Copy)
    v.wait_ge(S.s, n_bz)
    for h in range(2):
        V(v.tensor_scalar(T.rl[:, half(h)], T.colq16[:], f("an", h, h + 1), None, A.is_gt))
        V(v.tensor_scalar(T.rl[:, half(2 + h)], T.colq16[:], f("an", h, h + 1), None, A.is_equal))
    pe.wait_ge(S.v, cnt["v"])
    P(T.b0[:, 0:128], T.ident[:], T.posc[:], True, False)
    v.wait_ge(S.s, n_lw)
    for k, part in enumerate(("hh", "lw")):
        for h in range(2):
            a, b = 4 * k + 2 * h, 4 * k + 2 * h + 1
            V(v.tensor_scalar(T.ll[:, half(a)], T.ones[:], f(part, h, h + 1), None, A.mult))
            n = V(v.tensor_scalar(T.ll[:, half(b)], T.mrow[:], f("bz", h, h + 1), f(part, h, h + 1), A.is_ge, A.mult))
            pe.wait_ge(S.v, n)
            P(T.b0[:, 0:128], T.ll[:, half(a)], T.rl[:, half(h)], False, False)
            n = P(T.b0[:, 0:128], T.ll[:, half(b)], T.rl[:, half(2 + h)], False, k + h == 2)
    v.wait_ge(S.p, n)
    n_fu = V(v.tensor_copy(T.fu[:], T.b0[:, 0:128]))

    vv()
    v.wait_ge(S.s, n_self)
    v.wait_ge(S.landed, nland)
    sca.wait_ge(S.v, n_fu)
    ss()
    sca.wait_ge(S.landed, nland)
    ready = []
    for c in range(4):
        win = T.land[:, 0:8 * PAIR].indirect(T.fu[:, 32 * c:32 * c + 32])
        out = T.ys[:, 512 * c:512 * c + 512]
        if c % 2:
            ready.append(("s", C(out, win, AF.Copy)))
        else:
            ready.append(("v", V(v.tensor_copy(out, win))))
    for c, (q, n) in enumerate(ready):
        g.sync.wait_ge(S[q], n)
        g.sync.dma_start(T.y[:, 512 * c:512 * c + 512], T.ys[:, 512 * c:512 * c + 512]).then_inc(S.st, 16)

    g.wait_ge(S.v, n_hist)
    mine = T.lt[:, 4 * rank:4 * rank + 4]
    fused([([c for c in peers if c in ports], S.ht, mine, mine, on)])
    fused([([c for c in peers if c not in ports], S.ht, mine, mine, on)])
    xsend(1)
    if direct:
        g.wait_ge(S.ht, nht)
        blk = T.lt[:, 4 * r0:4 * r0 + 32]
        fused([(tdest(core, far), S.xt, blk, blk, off)])
    xsend(2)
    g.wait_ge(S.s, n_sl)
    send(first, S.sls if direct else S.rls, T.slx[:, 0:128], T.sl[:, 0:128], off)
    xsend(3)
    for part, c in calls:
        for t, d, m in c:
            for h in (0, 1):
                if part in (h, 2):
                    g.wait_ge(S[done[t, h][0]], done[t, h][1])
        fused([([d], S.landed, slot(7, part), slot(t, part), m) for t, d, m in c])
    g.wait_ge(S.sent, nsent[0])
    g.sync.wait_ge(S.st, 16 * len(ready))
    for q in ("gi", "v", "s", "p"):
        g.sync.wait_ge(S[q], cnt[q])
